import numpy as np
import ml_dtypes


def mxq(x, axis, fmt="e4m3"):
    dtype, down = {"e4m3": (ml_dtypes.float8_e4m3fn, 7), "e5m2": (ml_dtypes.float8_e5m2, 14)}[fmt]
    v = np.moveaxis(np.asarray(x, np.float32).astype(ml_dtypes.bfloat16).astype(np.float64), axis, -1)
    blocks = v.reshape(v.shape[:-1] + (-1, 32))
    amax = np.abs(blocks).max(-1, keepdims=True)
    byte = np.maximum(np.where(amax > 0, np.frexp(amax)[1] - 1 + 127, 0) - down, 1)
    scale = np.exp2(byte - 127.0)
    codes = (blocks / scale).astype(np.float32).astype(dtype).astype(np.float64)
    return np.moveaxis((codes * scale).reshape(v.shape), -1, axis)


WIDE = False


def mx_kscale(k):
    if not WIDE:
        return np.ones(k)
    levels = np.array([10, -10, 5, -5, 0])
    if k % 512:
        return np.exp2(np.random.permutation(np.resize(levels, k // 32))).repeat(32)
    a = np.empty((k // 512, 16))
    for p in range(k // 512):
        a[p, :8] = np.random.permutation(np.resize(levels, 8))
        for g in range(8):
            far = levels[np.abs(levels - a[p, g]) >= 10]
            a[p, g + 8] = far[np.random.randint(len(far))]
    return np.exp2(a.ravel()).repeat(32)


def f64(x):
    return np.asarray(x).astype(np.float64)


def striped(idx):
    return np.tile(idx.reshape(-1, 16).T, (8, 1)).astype(np.uint16)


def unstriped(offs):
    return offs[:16].T.reshape(-1).astype(np.int64)


E2M1 = np.array([0.0, 0.5, 1.0, 1.5, 2.0, 3.0, 4.0, 6.0, -0.0, -0.5, -1.0, -1.5, -2.0, -3.0, -4.0, -6.0])


def pack_weight(w, fmt):
    k, n = w.shape
    w = f64(np.asarray(w, np.float32).astype(ml_dtypes.bfloat16)).reshape(k // 32, 32, n)
    amax = np.abs(w).max(1)
    if fmt == "e4m3":
        byte = np.frexp(amax)[1] - 1 + 127 - 7
    else:
        mant, ex = np.frexp(amax / 6.0)
        byte = np.where(mant > 0.5, ex, ex - 1) + 127
    byte = np.clip(np.where(amax > 0, byte, 1), 1, 254)
    scaled = (w * np.exp2(127.0 - byte)[:, None, :]).reshape(k, n).astype(np.float32)
    by_word = np.ascontiguousarray(scaled.reshape(k // 512, 128, 4, n).transpose(0, 1, 3, 2))
    if fmt == "e4m3":
        words = by_word.astype(ml_dtypes.float8_e4m3fn).view(np.uint8)
    else:
        c = by_word.astype(ml_dtypes.float4_e2m1fn).view(np.uint8) & 0xF
        words = (c[..., 0::2] | (c[..., 1::2] << 4)).reshape(k // 512, 128, 2 * n)
    return np.ascontiguousarray(words), np.ascontiguousarray(byte.astype(np.uint8).reshape(k // 512, 16, n))


def unpack_weight(words, scales, fmt):
    g, _, n = scales.shape
    words = np.ascontiguousarray(words).reshape(g, 128, n, -1)
    if fmt == "e4m3":
        vals = words.view(ml_dtypes.float8_e4m3fn).astype(np.float64)
    else:
        nib = np.empty((g, 128, n, 4), np.uint8)
        nib[..., 0::2] = words & 0xF
        nib[..., 1::2] = words >> 4
        vals = E2M1[nib]
    vals = vals * np.repeat(np.exp2(scales.astype(np.float64) - 127.0), 8, axis=1)[..., None]
    return vals.transpose(0, 1, 3, 2).reshape(g * 512, n)


def gelu(v):
    return 0.5 * v * (1.0 + np.tanh(np.sqrt(2.0 / np.pi) * (v + 0.044715 * v**3)))


def bf(x):
    return np.asarray(x, np.float32).astype(ml_dtypes.bfloat16)


def planes(Y):
    n, m = Y.shape
    b = f64(bf(Y)).reshape(n // 32, 32, m)
    amax = np.abs(b).max(1)
    byte = np.clip(np.where(amax > 0, np.frexp(amax)[1] - 1 + 127 - 7, 1), 1, 254)
    codes = (b * np.exp2(127.0 - byte)[:, None, :]).reshape(n, m).astype(np.float32).astype(ml_dtypes.float8_e4m3fn).view(np.uint8)
    words = codes.reshape(n // 512, 128, 4, m).transpose(0, 1, 3, 2)
    return np.ascontiguousarray(words), np.ascontiguousarray(byte.astype(np.uint8).reshape(n // 512, 16, m))


K, T, S, H, P, N = 1536, 4096, 1024, 1024, 512, 1024

def setup_inputs():
    n = np.random.standard_normal
    s = mx_kscale(K)[:, None]
    u = mx_kscale(H)[:, None]
    tab_words, tab_scales = pack_weight(n((K, T)) * s, "e4m3")
    w1 = 0.9 * n((K, H)) / np.sqrt(K) / s
    w4 = n((H, N)) / np.sqrt(H) * np.exp(0.8 * n(N))[None, :] / u
    w4_words, w4_scales = pack_weight(w4, "e2m1")
    lean = np.sign(n(H)) * np.random.uniform(1.0, 3.0, H) * u[:, 0]
    mix = 4.0 * n((H, P)) * u
    return {
        "tab_words": tab_words, "tab_scales": tab_scales,
        "offs": striped(np.random.permutation(T)[:S]),
        "pos1": striped(np.random.permutation(S)[:P]),
        "pos2": striped(np.random.permutation(S)[:P]),
        "w1": w1.astype(np.float32),
        "temp": np.random.uniform(0.4, 1.6, H).astype(np.float32),
        "steep": np.random.uniform(1, 3, H).astype(np.float32),
        "share": np.random.uniform(0.1, 0.5, H).astype(np.float32),
        "lean": lean.astype(np.float32),
        "mix": mix.astype(np.float32),
        "w4_words": w4_words, "w4_scales": w4_scales,
        "reach": np.exp(0.5 * n((N, P))).astype(np.float32),
    }

def reference(tab_words, tab_scales, offs, pos1, pos2, w1, temp, steep, share, lean, mix, w4_words, w4_scales, reach):
    v = unpack_weight(tab_words, tab_scales, "e4m3")[:, unstriped(offs)]
    h = mxq(f64(w1), 0, "e4m3").T @ v
    top = h.max(axis=1)
    a = np.exp(f64(temp)[:, None] * (h[:, unstriped(pos1)] - top[:, None]))
    c = 1.0 / (1.0 + np.exp(-f64(steep)[:, None] * (h[:, unstriped(pos2)] - f64(share)[:, None] * top[:, None])))
    d = np.maximum(a, c) * f64(lean)[:, None] - np.minimum(a, c) * f64(mix)
    w4 = unpack_weight(w4_words, w4_scales, "e2m1")
    y = (w4.T @ mxq(d, 0, "e4m3")) * f64(reach)
    words, scales = planes(y)
    return y, words, scales

@@ -1,0 +1,346 @@
+from contextlib import ExitStack
+
+import concourse.mybir as mybir
+
+K, T, S, H, M, N = 1536, 4096, 1024, 1024, 512, 1024
+FLOPS = 2 * K * H * S + 2 * H * N * M
+
+F32 = mybir.dt.float32
+BF16 = mybir.dt.bfloat16
+I32 = mybir.dt.int32
+U32 = mybir.dt.uint32
+U16 = mybir.dt.uint16
+U8 = mybir.dt.uint8
+FP8X4 = mybir.dt.float8_e4m3fn_x4
+FP4X4 = mybir.dt.float4_e2m1fn_x4
+ALU = mybir.AluOpType
+ACT = mybir.ActivationFunctionType
+
+P = 128
+PACK = 4
+PASS = P * PACK
+K_PASSES = K // PASS
+R_GROUPS = H // PASS
+N_GROUPS = N // PASS
+BANK = 512
+HALF = M // 2
+QUADS = 4
+
+
+def tile_list_order_book_looks_kernel(
+    tc, tab_words, tab_scales, offs, pos1, pos2, w1, temp, steep, share, lean, mix,
+    w4_words, w4_scales, reach, out_0, out_1, out_2,
+):
+    nc = tc.nc
+    with ExitStack() as ctx:
+        keep = ctx.enter_context(tc.tile_pool(name="keep", bufs=1))
+        stage = ctx.enter_context(tc.tile_pool(name="stage", bufs=5))
+        work = ctx.enter_context(tc.tile_pool(name="work", bufs=2))
+        psum = ctx.enter_context(tc.psum_pool(name="psum", bufs=1))
+
+        def kept(shape, dtype, name):
+            return keep.tile(shape, dtype, name=name, align_bytes=64)
+
+        def staged(name):
+            return stage.tile([P, PACK, PASS], F32, name=name, tag="staged", align_bytes=64)
+
+        def tenant(tag, shape, name):
+            return keep.tile(shape, F32, name=name, tag=tag, align_bytes=64)
+
+        def bank(i, name):
+            return psum.tile([P, BANK], F32, name=name, tag="bank%d" % i)
+
+        offs_sb = keep.tile([P, S // 16], U16, name="offs_sb")
+        pos1_sb = keep.tile([P, M // 16], U16, name="pos1_sb")
+        pos2_sb = keep.tile([P, M // 16], U16, name="pos2_sb")
+
+        tab_sc = kept([P, T], U8, "tab_sc")
+        w4_sc_raw = kept([P, R_GROUPS, N], U8, "w4_sc_raw")
+        nc.vector.memset(tab_sc[:].bitcast(I32), 0)
+        nc.vector.memset(w4_sc_raw[:].bitcast(I32), 0)
+        rows = {}
+
+        def load_tab_scales(q):
+            nc.sync.dma_start(
+                out=tab_sc[32 * q : 32 * q + 4 * K_PASSES, :].bitcast(I32),
+                in_=tab_scales[:, 4 * q : 4 * q + 4, :].bitcast(I32),
+            )
+
+        def load_vector(name, vec):
+            rows[name] = kept([P, R_GROUPS * PACK], F32, name + "_sb")
+            nc.sync.dma_start(
+                out=rows[name][:].rearrange("p (b t) -> p b t", t=PACK),
+                in_=vec.rearrange("(b p t) -> p b t", p=P, t=PACK),
+            )
+
+        def load_w4_scales(q):
+            nc.sync.dma_start(
+                out=w4_sc_raw[32 * q : 32 * q + 4, :, :].bitcast(I32),
+                in_=w4_scales[:, 4 * q : 4 * q + 4, :].rearrange("b r n -> r b n").bitcast(I32),
+            )
+
+        w1_raw, tab, got = {}, {}, {}
+
+        def load_w1(a, b):
+            w1_raw[a, b] = staged("w1_raw")
+            nc.sync.dma_start(
+                out=w1_raw[a, b][:],
+                in_=w1[a * PASS : (a + 1) * PASS, b * PASS : (b + 1) * PASS].rearrange("(p j) c -> p j c", j=PACK),
+            )
+
+        def load_tab(a):
+            tab[a] = kept([P, T], I32, "tab%d" % a)
+            nc.sync.dma_start(out=tab[a][:], in_=tab_words[a].rearrange("p t i -> p (t i)").bitcast(I32))
+
+        def load_rows(src, b, name):
+            dst = staged(name)
+            nc.sync.dma_start(out=dst[:], in_=src[b * PASS : (b + 1) * PASS, :].rearrange("(p t) m -> p t m", t=PACK))
+            return dst
+
+        def gather_words(a):
+            got[a] = kept([P, S], U32, "got%d" % a)
+            nc.vector.tensor_copy(got[a][:], tab[a][:].bitcast(U32).indirect(offs_sb[:]))
+
+        w1_q, w1_s = {}, {}
+
+        def quantise_w1(a, b, scalar_cols):
+            grouped = work.tile([P, PASS * PACK], BF16, name="w1_grouped", align_bytes=64)
+            dst = grouped[:].rearrange("p (t m j) -> p m j t", t=PACK, j=PACK)
+            src = w1_raw[a, b][:].rearrange("p j (m t) -> p m j t", t=PACK)
+            if scalar_cols > 0:
+                nc.scalar.activation(out=dst[:, :scalar_cols], in_=src[:, :scalar_cols], func=ACT.Copy)
+            if scalar_cols < P:
+                nc.vector.tensor_copy(out=dst[:, scalar_cols:], in_=src[:, scalar_cols:])
+            w1_q[a, b] = kept([P, PASS], U32, "w1_q%d%d" % (a, b))
+            w1_s[a, b] = kept([P, PASS], U8, "w1_s%d%d" % (a, b))
+            nc.vector.quantize_mx(out=w1_q[a, b][:].bitcast(FP8X4), scales=w1_s[a, b][:], in_=grouped[:])
+
+        acc1 = {}
+        pair_order = [(t0 + dt, half) for t0 in (0, 2) for half in (0, 1) for dt in (0, 1)]
+
+        def first_product(passes, b):
+            for t, half, a in [(t, half, a) for t, half in pair_order for a in passes]:
+                if a == 0:
+                    acc1[b, t, half] = bank(2 * t + half, "acc1")
+                cols = slice(half * BANK, (half + 1) * BANK)
+                nc.tensor.matmul_mx(
+                    out=acc1[b, t, half][:],
+                    lhsT=w1_q[a, b][:, t * P : (t + 1) * P].bitcast(FP8X4),
+                    lhsT_scale=w1_s[a, b][:, t * P : (t + 1) * P],
+                    rhs=got[a][:, cols].bitcast(FP8X4),
+                    rhs_scale=got_sc[4 * a : P, cols],
+                    start=(a == 0),
+                    stop=(a == K_PASSES - 1),
+                )
+
+        h = {}
+        top_half = kept([P, R_GROUPS * PACK], F32, "top_half")
+        top = kept([P, R_GROUPS * PACK], F32, "top")
+
+        bias = {}
+
+        def leave_psum(b, first, second):
+            first_factor = factor[first]
+            first_bias = tenant("look%s%d" % (second == ACT.Exp, b), [P, PACK], "first_bias")
+            bias[first, b] = first_bias
+            for t, half in pair_order:
+                col = slice(b * PACK + t, b * PACK + t + 1)
+                if half == 0:
+                    h[b, t] = keep.tile([P, S], F32, name="h", tag="h%d%d" % (b, t), align_bytes=64)
+                nc.vector.tensor_scalar(
+                    out=h[b, t][:, half * BANK : (half + 1) * BANK],
+                    in0=acc1[b, t, half][:],
+                    scalar1=1.0,
+                    scalar2=top_half[:, col] if half else None,
+                    op0=ALU.mult,
+                    op1=ALU.max,
+                    accum_out=top[:, col] if half else top_half[:, col],
+                )
+                if half:
+                    nc.gpsimd.tensor_scalar(
+                        out=first_bias[:, t : t + 1], in0=first_factor[:, col], scalar1=top[:, col], scalar2=0.0,
+                        op0=ALU.mult, op1=ALU.add,
+                    )
+            group = slice(b * PACK, (b + 1) * PACK)
+            bias[second, b] = kept([P, PACK], F32, "second_bias%d" % b)
+            nc.gpsimd.tensor_tensor(out=bias[second, b][:], in0=factor[second][:, group], in1=top[:, group], op=ALU.mult)
+
+        looked = {}
+
+        def look(func, b, width):
+            scale, pos = (rows["temp"], pos1_sb) if func == ACT.Exp else (rows["steep"], pos2_sb)
+            looked[func, b] = tenant("look%s%d" % (func == ACT.Exp, b), [P, PACK, M], "looked")
+            for m0 in range(0, M, width):
+                for t in range(PACK):
+                    nc.scalar.activation(
+                        out=looked[func, b][:, t, m0 : m0 + width],
+                        in_=h[b, t][:].indirect(pos[:, m0 // 16 : (m0 + width) // 16]),
+                        func=func,
+                        bias=bias[func, b][:, t : t + 1],
+                        scale=scale[:, b * PACK + t : b * PACK + t + 1],
+                    )
+
+        d_rows = {}
+
+        def combine(b, half):
+            cols = slice(half * HALF, (half + 1) * HALF)
+            early, late = looked[ACT.Exp, b][:, :, cols], looked[ACT.Sigmoid, b][:, :, cols]
+            low = work.tile([P, PACK, HALF], F32, name="low", align_bytes=64)
+            pairs = (slice(0, 2), slice(2, 4))
+            for ts in pairs:
+                nc.vector.tensor_tensor(out=low[:, ts, :], in0=early[:, ts, :], in1=late[:, ts, :], op=ALU.min)
+            for ts in pairs:
+                nc.vector.tensor_tensor(out=early[:, ts, :], in0=early[:, ts, :], in1=late[:, ts, :], op=ALU.max)
+            for ts in pairs:
+                nc.vector.tensor_tensor(out=low[:, ts, :], in0=low[:, ts, :], in1=mix_sb[b][:, ts, cols], op=ALU.mult)
+            d_rows[b, half] = work.tile([P, PACK, HALF], BF16, name="d_rows", align_bytes=64)
+            for t in range(PACK):
+                nc.vector.scalar_tensor_tensor(
+                    out=d_rows[b, half][:, t, :],
+                    in0=early[:, t, :],
+                    scalar=rows["lean"][:, b * PACK + t : b * PACK + t + 1],
+                    in1=low[:, t, :],
+                    op0=ALU.mult,
+                    op1=ALU.subtract,
+                )
+
+        def interleave(src, copy):
+            grouped = work.tile([P, HALF * PACK], BF16, name="grouped", bufs=3, align_bytes=64)
+            copy(
+                out=grouped[:].rearrange("p (c i t) -> p c t i", i=4, t=PACK),
+                in_=src.rearrange("p t (c i) -> p c t i", i=4),
+            )
+            return grouped
+
+        acc2 = {}
+
+        def second_product(b, half):
+            grouped = interleave(d_rows[b, half][:], nc.scalar.copy)
+            d_q = kept([P, HALF], U32, "d_q%d%d" % (b, half))
+            d_s = kept([P, HALF], U8, "d_s%d%d" % (b, half))
+            nc.vector.quantize_mx(out=d_q[:].bitcast(FP8X4), scales=d_s[:], in_=grouped[:])
+            for g in range(N_GROUPS):
+                for t in range(PACK):
+                    if b == 0 and t % 2 == 0:
+                        acc2[half, g, t // 2] = bank(4 * half + 2 * g + t // 2, "acc2")
+                    c0 = ((b * N_GROUPS + g) * PACK + t) * P
+                    nc.tensor.matmul_mx(
+                        out=acc2[half, g, t // 2][:, (t % 2) * HALF : (t % 2 + 1) * HALF],
+                        lhsT=w4_w[:, 2 * c0 : 2 * (c0 + P)].bitcast(FP4X4),
+                        lhsT_scale=w4_sc[:, c0 : c0 + P],
+                        rhs=d_q[:].bitcast(FP8X4),
+                        rhs_scale=d_s[:],
+                        start=(b == 0 and t % 2 == 0),
+                        stop=(b == R_GROUPS - 1 and t % 2 == 1),
+                    )
+
+        y_s = kept([P, N_GROUPS, M], U8, "y_s")
+
+        y_half = {}
+
+        def finish(half, g, copy):
+            cols = slice(half * HALF, (half + 1) * HALF)
+            if g == 0:
+                y_half[half] = tenant("look%s0" % (half == 0), [P, N_GROUPS, PACK, HALF], "y")
+            y = y_half[half][:, g, :, :]
+            for tp in (0, 1):
+                nc.vector.tensor_tensor(
+                    out=y[:, 2 * tp : 2 * tp + 2, :],
+                    in0=acc2[half, g, tp][:].rearrange("p (t m) -> p t m", t=2),
+                    in1=reach_sb[g][:, 2 * tp : 2 * tp + 2, cols],
+                    op=ALU.mult,
+                )
+            nc.sync.dma_start(
+                out=out_0[g * PASS : (g + 1) * PASS, cols].rearrange("(p t) m -> p t m", t=PACK), in_=y
+            )
+            grouped = interleave(y, copy)
+            y_q = kept([P, HALF], I32, "y_q%d%d" % (half, g))
+            nc.vector.quantize_mx(out=y_q[:].bitcast(FP8X4), scales=y_s[:, g, cols], in_=grouped[:])
+            nc.sync.dma_start(out=out_1[g, :, cols, :].rearrange("p m t -> p (m t)").bitcast(I32), in_=y_q[:])
+
+        load_w1(0, 0)
+        nc.sync.dma_start(offs_sb[:], offs)
+        load_vector("temp", temp)
+        load_vector("steep", steep)
+        load_vector("share", share)
+        load_tab(0)
+        load_w1(1, 0)
+        nc.sync.dma_start(pos1_sb[:], pos1)
+        for q in range(QUADS):
+            load_tab_scales(q)
+        load_tab(1)
+        for q in range(QUADS):
+            load_w4_scales(q)
+        load_tab(2)
+        load_w1(2, 0)
+        nc.sync.dma_start(pos2_sb[:], pos2)
+        load_w1(0, 1)
+        load_w1(1, 1)
+
+        got_sc = kept([P, S], U8, "got_sc")
+        nc.vector.tensor_copy(got_sc[:], tab_sc[:].indirect(offs_sb[:]))
+        quantise_w1(0, 0, P)
+        gather_words(0)
+        first_product([0], 0)
+        quantise_w1(1, 0, P)
+        gather_words(1)
+        first_product([1], 0)
+
+        neg_temp = kept([P, R_GROUPS * PACK], F32, "neg_temp")
+        neg_gate = kept([P, R_GROUPS * PACK], F32, "neg_gate")
+        nc.vector.tensor_scalar(out=neg_temp[:], in0=rows["temp"][:], scalar1=-1.0, scalar2=None, op0=ALU.mult)
+        nc.vector.scalar_tensor_tensor(
+            out=neg_gate[:], in0=rows["steep"][:], scalar=-1.0, in1=rows["share"][:], op0=ALU.mult, op1=ALU.mult
+        )
+
+        w4_sc = kept([P, R_GROUPS * N], U8, "w4_sc")
+        nc.vector.tensor_copy(
+            out=w4_sc[:].rearrange("p (c t q) -> p c t q", t=PACK, q=P),
+            in_=w4_sc_raw[:].rearrange("p b (g q t) -> p (b g) t q", t=PACK, q=P),
+        )
+        gather_words(2)
+        quantise_w1(2, 0, 48)
+        first_product([2], 0)
+
+        load_w1(2, 1)
+        load_vector("lean", lean)
+        mix_sb = [load_rows(mix, b, "mix_sb") for b in range(R_GROUPS)]
+        w4_raw = kept([P, R_GROUPS, 2 * N], U8, "w4_raw")
+        nc.sync.dma_start(out=w4_raw[:].bitcast(I32), in_=w4_words.rearrange("b p n -> p b n").bitcast(I32))
+        reach_sb = [load_rows(reach, g, "reach_sb") for g in range(N_GROUPS)]
+
+        factor = {ACT.Exp: neg_temp, ACT.Sigmoid: neg_gate}
+        leave_psum(0, ACT.Exp, ACT.Sigmoid)
+        quantise_w1(0, 1, P)
+        look(ACT.Exp, 0, M)
+        first_product([0], 1)
+        quantise_w1(1, 1, 0)
+        quantise_w1(2, 1, 0)
+        first_product([1, 2], 1)
+        look(ACT.Sigmoid, 0, M)
+        leave_psum(1, ACT.Sigmoid, ACT.Exp)
+        look(ACT.Sigmoid, 1, M)
+        combine(0, 0)
+        combine(0, 1)
+        look(ACT.Exp, 1, HALF)
+
+        w4_w = keep.tile([P, R_GROUPS * 2 * N], U8, name="w4_w", tag="h13", align_bytes=64)
+        nc.scalar.copy(
+            out=w4_w[:].bitcast(U16).rearrange("p (c t q) -> p c q t", t=PACK, q=P),
+            in_=w4_raw[:].bitcast(U16).rearrange("p b (g q t) -> p (b g) q t", t=PACK, q=P),
+        )
+        combine(1, 0)
+        second_product(0, 0)
+        second_product(1, 0)
+        second_product(0, 1)
+        combine(1, 1)
+        finish(0, 0, nc.scalar.copy)
+        second_product(1, 1)
+        finish(0, 1, nc.scalar.copy)
+        finish(1, 0, nc.scalar.copy)
+        finish(1, 1, nc.vector.tensor_copy)
+        for q in range(QUADS):
+            nc.sync.dma_start(
+                out=out_2[:, 4 * q : 4 * q + 4, :].rearrange("g r m -> r g m").bitcast(I32),
+                in_=y_s[32 * q : 32 * q + 4, :, :].bitcast(I32),
+            )

@@ -103,17 +103,21 @@ def tile_list_order_book_looks_kernel(
 
         w1_q, w1_s = {}, {}
 
-        def quantise_w1(a, b, scalar_cols):
-            grouped = work.tile([P, PASS * PACK], BF16, name="w1_grouped", align_bytes=64)
-            dst = grouped[:].rearrange("p (t m j) -> p m j t", t=PACK, j=PACK)
-            src = w1_raw[a, b][:].rearrange("p j (m t) -> p m j t", t=PACK)
+        w1_grouped = {}
+
+        def round_w1(a, b, scalar_cols):
+            grouped = w1_grouped[a, b] = work.tile([P, PASS * PACK], BF16, name="w1_grouped", align_bytes=64)
+            dst = grouped[:].rearrange("p (t m j) -> p m t j", t=PACK, j=PACK)
+            src = w1_raw[a, b][:].rearrange("p j (m t) -> p m t j", t=PACK)
             if scalar_cols > 0:
                 nc.scalar.activation(out=dst[:, :scalar_cols], in_=src[:, :scalar_cols], func=ACT.Copy)
             if scalar_cols < P:
                 nc.vector.tensor_copy(out=dst[:, scalar_cols:], in_=src[:, scalar_cols:])
+
+        def quantise_w1(a, b):
             w1_q[a, b] = kept([P, PASS], U32, "w1_q%d%d" % (a, b))
             w1_s[a, b] = kept([P, PASS], U8, "w1_s%d%d" % (a, b))
-            nc.vector.quantize_mx(out=w1_q[a, b][:].bitcast(FP8X4), scales=w1_s[a, b][:], in_=grouped[:])
+            nc.vector.quantize_mx(out=w1_q[a, b][:].bitcast(FP8X4), scales=w1_s[a, b][:], in_=w1_grouped[a, b][:])
 
         acc1 = {}
         pair_order = [(t0 + dt, half) for t0 in (0, 2) for half in (0, 1) for dt in (0, 1)]
@@ -134,16 +138,16 @@ def tile_list_order_book_looks_kernel(
                 )
 
         h = {}
-        top_half = kept([P, R_GROUPS * PACK], F32, "top_half")
         top = kept([P, R_GROUPS * PACK], F32, "top")
 
-        bias = {}
+        bias, top_half = {}, {}
 
-        def leave_psum(b, first, second):
-            first_factor = factor[first]
-            first_bias = tenant("look%s%d" % (second == ACT.Exp, b), [P, PACK], "first_bias")
-            bias[first, b] = first_bias
-            for t, half in pair_order:
+        def leave_psum(b, first, banks):
+            second = ACT.Sigmoid if first == ACT.Exp else ACT.Exp
+            for t, half in banks:
+                if (t, half) == (0, 0):
+                    bias[first, b] = tenant("look%s%d" % (second == ACT.Exp, b), [P, PACK], "first_bias")
+                    top_half[b] = tenant("low", [P, PACK], "top_half")
                 col = slice(b * PACK + t, b * PACK + t + 1)
                 if half == 0:
                     h[b, t] = keep.tile([P, S], F32, name="h", tag="h%d%d" % (b, t), align_bytes=64)
@@ -151,19 +155,21 @@ def tile_list_order_book_looks_kernel(
                     out=h[b, t][:, half * BANK : (half + 1) * BANK],
                     in0=acc1[b, t, half][:],
                     scalar1=1.0,
-                    scalar2=top_half[:, col] if half else None,
+                    scalar2=top_half[b][:, t : t + 1] if half else None,
                     op0=ALU.mult,
                     op1=ALU.max,
-                    accum_out=top[:, col] if half else top_half[:, col],
+                    accum_out=top[:, col] if half else top_half[b][:, t : t + 1],
                 )
-                if half:
-                    nc.gpsimd.tensor_scalar(
-                        out=first_bias[:, t : t + 1], in0=first_factor[:, col], scalar1=top[:, col], scalar2=0.0,
-                        op0=ALU.mult, op1=ALU.add,
+                if half and b == 0:
+                    nc.scalar.activation(
+                        out=bias[first, b][:, t : t + 1], in_=factor[first][:, col], func=ACT.Copy, scale=top[:, col]
                     )
-            group = slice(b * PACK, (b + 1) * PACK)
-            bias[second, b] = kept([P, PACK], F32, "second_bias%d" % b)
-            nc.gpsimd.tensor_tensor(out=bias[second, b][:], in0=factor[second][:, group], in1=top[:, group], op=ALU.mult)
+
+        def vector_bias(b, func, t0, t1):
+            if (func, b) not in bias:
+                bias[func, b] = kept([P, PACK], F32, "second_bias%d" % b)
+            group = slice(b * PACK + t0, b * PACK + t1)
+            nc.vector.tensor_tensor(out=bias[func, b][:, t0:t1], in0=factor[func][:, group], in1=top[:, group], op=ALU.mult)
 
         looked = {}
 
@@ -181,25 +187,32 @@ def tile_list_order_book_looks_kernel(
                     )
 
         d_rows = {}
+        halves = (slice(0, HALF), slice(HALF, M))
 
-        def combine(b, half):
-            cols = slice(half * HALF, (half + 1) * HALF)
-            early, late = looked[ACT.Exp, b][:, :, cols], looked[ACT.Sigmoid, b][:, :, cols]
-            low = work.tile([P, PACK, HALF], F32, name="low", align_bytes=64)
-            pairs = (slice(0, 2), slice(2, 4))
+        low = {}
+        pairs = (slice(0, 2), slice(2, 4))
+
+        def order_looks(b, cols):
+            if cols.start == 0:
+                low[b] = tenant("low", [P, PACK, M], "low")
+                d_rows[b] = kept([P, PACK, M], BF16, "d_rows%d" % b)
+            early, late = looked[ACT.Exp, b], looked[ACT.Sigmoid, b]
             for ts in pairs:
-                nc.vector.tensor_tensor(out=low[:, ts, :], in0=early[:, ts, :], in1=late[:, ts, :], op=ALU.min)
+                nc.vector.tensor_tensor(out=low[b][:, ts, cols], in0=early[:, ts, cols], in1=late[:, ts, cols], op=ALU.min)
             for ts in pairs:
-                nc.vector.tensor_tensor(out=early[:, ts, :], in0=early[:, ts, :], in1=late[:, ts, :], op=ALU.max)
+                nc.vector.tensor_tensor(out=early[:, ts, cols], in0=early[:, ts, cols], in1=late[:, ts, cols], op=ALU.max)
+
+        def combine(b, cols):
             for ts in pairs:
-                nc.vector.tensor_tensor(out=low[:, ts, :], in0=low[:, ts, :], in1=mix_sb[b][:, ts, cols], op=ALU.mult)
-            d_rows[b, half] = work.tile([P, PACK, HALF], BF16, name="d_rows", align_bytes=64)
+                nc.vector.tensor_tensor(
+                    out=low[b][:, ts, cols], in0=low[b][:, ts, cols], in1=mix_sb[b][:, ts, cols], op=ALU.mult
+                )
             for t in range(PACK):
                 nc.vector.scalar_tensor_tensor(
-                    out=d_rows[b, half][:, t, :],
-                    in0=early[:, t, :],
+                    out=d_rows[b][:, t, cols],
+                    in0=looked[ACT.Exp, b][:, t, cols],
                     scalar=rows["lean"][:, b * PACK + t : b * PACK + t + 1],
-                    in1=low[:, t, :],
+                    in1=low[b][:, t, cols],
                     op0=ALU.mult,
                     op1=ALU.subtract,
                 )
@@ -214,25 +227,28 @@ def tile_list_order_book_looks_kernel(
 
         acc2 = {}
 
-        def second_product(b, half):
-            grouped = interleave(d_rows[b, half][:], nc.scalar.copy)
-            d_q = kept([P, HALF], U32, "d_q%d%d" % (b, half))
-            d_s = kept([P, HALF], U8, "d_s%d%d" % (b, half))
-            nc.vector.quantize_mx(out=d_q[:].bitcast(FP8X4), scales=d_s[:], in_=grouped[:])
-            for g in range(N_GROUPS):
-                for t in range(PACK):
-                    if b == 0 and t % 2 == 0:
-                        acc2[half, g, t // 2] = bank(4 * half + 2 * g + t // 2, "acc2")
-                    c0 = ((b * N_GROUPS + g) * PACK + t) * P
-                    nc.tensor.matmul_mx(
-                        out=acc2[half, g, t // 2][:, (t % 2) * HALF : (t % 2 + 1) * HALF],
-                        lhsT=w4_w[:, 2 * c0 : 2 * (c0 + P)].bitcast(FP4X4),
-                        lhsT_scale=w4_sc[:, c0 : c0 + P],
-                        rhs=d_q[:].bitcast(FP8X4),
-                        rhs_scale=d_s[:],
-                        start=(b == 0 and t % 2 == 0),
-                        stop=(b == R_GROUPS - 1 and t % 2 == 1),
-                    )
+        d_q, d_s = {}, {}
+
+        def quantise_d(b, half):
+            grouped = interleave(d_rows[b][:, :, halves[half]], nc.scalar.copy)
+            d_q[b, half] = kept([P, HALF], U32, "d_q%d%d" % (b, half))
+            d_s[b, half] = kept([P, HALF], U8, "d_s%d%d" % (b, half))
+            nc.vector.quantize_mx(out=d_q[b, half][:].bitcast(FP8X4), scales=d_s[b, half][:], in_=grouped[:])
+
+        def second_product(b, half, g):
+            for t in range(PACK):
+                if b == 0 and t % 2 == 0:
+                    acc2[half, g, t // 2] = bank(4 * half + 2 * g + t // 2, "acc2")
+                c0 = ((b * N_GROUPS + g) * PACK + t) * P
+                nc.tensor.matmul_mx(
+                    out=acc2[half, g, t // 2][:, (t % 2) * HALF : (t % 2 + 1) * HALF],
+                    lhsT=w4_w[:, 2 * c0 : 2 * (c0 + P)].bitcast(FP4X4),
+                    lhsT_scale=w4_sc[:, c0 : c0 + P],
+                    rhs=d_q[b, half][:].bitcast(FP8X4),
+                    rhs_scale=d_s[b, half][:],
+                    start=(b == 0 and t % 2 == 0),
+                    stop=(b == R_GROUPS - 1 and t % 2 == 1),
+                )
 
         y_s = kept([P, N_GROUPS, M], U8, "y_s")
 
@@ -263,26 +279,40 @@ def tile_list_order_book_looks_kernel(
         load_vector("temp", temp)
         load_vector("steep", steep)
         load_vector("share", share)
-        load_tab(0)
-        load_w1(1, 0)
         nc.sync.dma_start(pos1_sb[:], pos1)
+        nc.sync.dma_start(pos2_sb[:], pos2)
+        load_tab(0)
         for q in range(QUADS):
             load_tab_scales(q)
-        load_tab(1)
+        load_w1(1, 0)
         for q in range(QUADS):
             load_w4_scales(q)
+        w4_raw = keep.tile([P, R_GROUPS, 2 * N], U8, name="w4_raw", tag="lookTrue0", align_bytes=64)
+        nc.sync.dma_start(out=w4_raw[:].bitcast(I32), in_=w4_words.rearrange("b p n -> p b n").bitcast(I32))
+        load_tab(1)
         load_tab(2)
         load_w1(2, 0)
-        nc.sync.dma_start(pos2_sb[:], pos2)
         load_w1(0, 1)
         load_w1(1, 1)
 
         got_sc = kept([P, S], U8, "got_sc")
         nc.vector.tensor_copy(got_sc[:], tab_sc[:].indirect(offs_sb[:]))
-        quantise_w1(0, 0, P)
+        round_w1(0, 0, P)
+        quantise_w1(0, 0)
         gather_words(0)
         first_product([0], 0)
-        quantise_w1(1, 0, P)
+        round_w1(1, 0, P)
+        quantise_w1(1, 0)
+        w4_sc = kept([P, R_GROUPS * N], U8, "w4_sc")
+        nc.vector.tensor_copy(
+            out=w4_sc[:].rearrange("p (c t q) -> p c t q", t=PACK, q=P),
+            in_=w4_sc_raw[:].rearrange("p b (g q t) -> p (b g) t q", t=PACK, q=P),
+        )
+        w4_w = kept([P, R_GROUPS * 2 * N], U8, "w4_w")
+        nc.scalar.copy(
+            out=w4_w[:].bitcast(U16).rearrange("p (c t q i) -> p c q t i", t=PACK, q=16, i=8),
+            in_=w4_raw[:].bitcast(U16).rearrange("p b (g q i t) -> p (b g) q t i", t=PACK, q=16, i=8),
+        )
         gather_words(1)
         first_product([1], 0)
 
@@ -293,49 +323,58 @@ def tile_list_order_book_looks_kernel(
             out=neg_gate[:], in0=rows["steep"][:], scalar=-1.0, in1=rows["share"][:], op0=ALU.mult, op1=ALU.mult
         )
 
-        w4_sc = kept([P, R_GROUPS * N], U8, "w4_sc")
-        nc.vector.tensor_copy(
-            out=w4_sc[:].rearrange("p (c t q) -> p c t q", t=PACK, q=P),
-            in_=w4_sc_raw[:].rearrange("p b (g q t) -> p (b g) t q", t=PACK, q=P),
-        )
         gather_words(2)
-        quantise_w1(2, 0, 48)
+        round_w1(2, 0, 48)
+        quantise_w1(2, 0)
         first_product([2], 0)
 
         load_w1(2, 1)
         load_vector("lean", lean)
         mix_sb = [load_rows(mix, b, "mix_sb") for b in range(R_GROUPS)]
-        w4_raw = kept([P, R_GROUPS, 2 * N], U8, "w4_raw")
-        nc.sync.dma_start(out=w4_raw[:].bitcast(I32), in_=w4_words.rearrange("b p n -> p b n").bitcast(I32))
         reach_sb = [load_rows(reach, g, "reach_sb") for g in range(N_GROUPS)]
 
         factor = {ACT.Exp: neg_temp, ACT.Sigmoid: neg_gate}
-        leave_psum(0, ACT.Exp, ACT.Sigmoid)
-        quantise_w1(0, 1, P)
+        round_w1(0, 1, P)
+        leave_psum(0, ACT.Exp, pair_order[:4])
+        quantise_w1(0, 1)
+        leave_psum(0, ACT.Exp, pair_order[4:7])
+        round_w1(1, 1, 0)
+        leave_psum(0, ACT.Exp, pair_order[7:])
         look(ACT.Exp, 0, M)
         first_product([0], 1)
-        quantise_w1(1, 1, 0)
-        quantise_w1(2, 1, 0)
-        first_product([1, 2], 1)
+        quantise_w1(1, 1)
+        first_product([1], 1)
+        round_w1(2, 1, 0)
+        vector_bias(0, ACT.Sigmoid, 0, PACK)
+        quantise_w1(2, 1)
+        first_product([2], 1)
         look(ACT.Sigmoid, 0, M)
-        leave_psum(1, ACT.Sigmoid, ACT.Exp)
+        leave_psum(1, ACT.Sigmoid, pair_order[:5])
+        vector_bias(1, ACT.Sigmoid, 0, 2)
+        leave_psum(1, ACT.Sigmoid, pair_order[5:])
+        vector_bias(1, ACT.Sigmoid, 2, PACK)
+        vector_bias(1, ACT.Exp, 0, PACK)
         look(ACT.Sigmoid, 1, M)
-        combine(0, 0)
-        combine(0, 1)
+        order_looks(0, slice(0, M))
+        combine(0, slice(0, M))
         look(ACT.Exp, 1, HALF)
 
-        w4_w = keep.tile([P, R_GROUPS * 2 * N], U8, name="w4_w", tag="h13", align_bytes=64)
-        nc.scalar.copy(
-            out=w4_w[:].bitcast(U16).rearrange("p (c t q) -> p c q t", t=PACK, q=P),
-            in_=w4_raw[:].bitcast(U16).rearrange("p b (g q t) -> p (b g) q t", t=PACK, q=P),
-        )
-        combine(1, 0)
-        second_product(0, 0)
-        second_product(1, 0)
-        second_product(0, 1)
-        combine(1, 1)
+        order_looks(1, halves[0])
+        combine(1, halves[0])
+        order_looks(1, halves[1])
+        quantise_d(0, 0)
+        quantise_d(1, 0)
+        for g in range(N_GROUPS):
+            for b in range(R_GROUPS):
+                second_product(b, 0, g)
+        combine(1, halves[1])
+        quantise_d(0, 1)
+        for g in range(N_GROUPS):
+            second_product(0, 1, g)
         finish(0, 0, nc.scalar.copy)
-        second_product(1, 1)
+        quantise_d(1, 1)
+        for g in range(N_GROUPS):
+            second_product(1, 1, g)
         finish(0, 1, nc.scalar.copy)
         finish(1, 0, nc.scalar.copy)
         finish(1, 1, nc.vector.tensor_copy)

@@ -56,12 +56,12 @@ def tile_list_order_book_looks_kernel(
 
         tab_sc = kept([P, T], U8, "tab_sc")
         w4_sc_raw = kept([P, R_GROUPS, N], U8, "w4_sc_raw")
-        nc.vector.memset(tab_sc[:].bitcast(I32), 0)
+        nc.gpsimd.memset(tab_sc[:].bitcast(I32), 0)
         nc.vector.memset(w4_sc_raw[:].bitcast(I32), 0)
         rows = {}
 
         def load_tab_scales(q):
-            nc.sync.dma_start(
+            nc.gpsimd.dma_start(
                 out=tab_sc[32 * q : 32 * q + 4 * K_PASSES, :].bitcast(I32),
                 in_=tab_scales[:, 4 * q : 4 * q + 4, :].bitcast(I32),
             )
@@ -97,9 +97,13 @@ def tile_list_order_book_looks_kernel(
             nc.sync.dma_start(out=dst[:], in_=src[b * PASS : (b + 1) * PASS, :].rearrange("(p t) m -> p t m", t=PACK))
             return dst
 
-        def gather_words(a):
+        def gather_words(a, width):
             got[a] = kept([P, S], U32, "got%d" % a)
-            nc.vector.tensor_copy(got[a][:], tab[a][:].bitcast(U32).indirect(offs_sb[:]))
+            for s0 in range(0, S, width):
+                nc.vector.tensor_copy(
+                    got[a][:, s0 : s0 + width],
+                    tab[a][:].bitcast(U32).indirect(offs_sb[:, s0 // 16 : (s0 + width) // 16]),
+                )
 
         w1_q, w1_s = {}, {}
 
@@ -274,6 +278,8 @@ def tile_list_order_book_looks_kernel(
             nc.vector.quantize_mx(out=y_q[:].bitcast(FP8X4), scales=y_s[:, g, cols], in_=grouped[:])
             nc.sync.dma_start(out=out_1[g, :, cols, :].rearrange("p m t -> p (m t)").bitcast(I32), in_=y_q[:])
 
+        for q in range(QUADS):
+            load_tab_scales(q)
         load_w1(0, 0)
         nc.sync.dma_start(offs_sb[:], offs)
         load_vector("temp", temp)
@@ -282,40 +288,25 @@ def tile_list_order_book_looks_kernel(
         nc.sync.dma_start(pos1_sb[:], pos1)
         nc.sync.dma_start(pos2_sb[:], pos2)
         load_tab(0)
-        for q in range(QUADS):
-            load_tab_scales(q)
         load_w1(1, 0)
         for q in range(QUADS):
             load_w4_scales(q)
-        w4_raw = keep.tile([P, R_GROUPS, 2 * N], U8, name="w4_raw", tag="lookTrue0", align_bytes=64)
-        nc.sync.dma_start(out=w4_raw[:].bitcast(I32), in_=w4_words.rearrange("b p n -> p b n").bitcast(I32))
         load_tab(1)
-        load_tab(2)
         load_w1(2, 0)
         load_w1(0, 1)
+        w4_raw = keep.tile([P, R_GROUPS, 2 * N], U8, name="w4_raw", tag="lookTrue0", align_bytes=64)
+        nc.sync.dma_start(out=w4_raw[:].bitcast(I32), in_=w4_words.rearrange("b p n -> p b n").bitcast(I32))
+        load_tab(2)
         load_w1(1, 1)
 
         got_sc = kept([P, S], U8, "got_sc")
-        nc.vector.tensor_copy(got_sc[:], tab_sc[:].indirect(offs_sb[:]))
         round_w1(0, 0, P)
         quantise_w1(0, 0)
-        gather_words(0)
+        load_w1(2, 1)
+        load_vector("lean", lean)
+        gather_words(0, S)
+        nc.vector.tensor_copy(got_sc[:], tab_sc[:].indirect(offs_sb[:]))
         first_product([0], 0)
-        round_w1(1, 0, P)
-        quantise_w1(1, 0)
-        w4_sc = kept([P, R_GROUPS * N], U8, "w4_sc")
-        nc.vector.tensor_copy(
-            out=w4_sc[:].rearrange("p (c t q) -> p c t q", t=PACK, q=P),
-            in_=w4_sc_raw[:].rearrange("p b (g q t) -> p (b g) t q", t=PACK, q=P),
-        )
-        w4_w = kept([P, R_GROUPS * 2 * N], U8, "w4_w")
-        nc.scalar.copy(
-            out=w4_w[:].bitcast(U16).rearrange("p (c t q i) -> p c q t i", t=PACK, q=16, i=8),
-            in_=w4_raw[:].bitcast(U16).rearrange("p b (g q i t) -> p (b g) q t i", t=PACK, q=16, i=8),
-        )
-        gather_words(1)
-        first_product([1], 0)
-
         neg_temp = kept([P, R_GROUPS * PACK], F32, "neg_temp")
         neg_gate = kept([P, R_GROUPS * PACK], F32, "neg_gate")
         nc.vector.tensor_scalar(out=neg_temp[:], in0=rows["temp"][:], scalar1=-1.0, scalar2=None, op0=ALU.mult)
@@ -323,36 +314,45 @@ def tile_list_order_book_looks_kernel(
             out=neg_gate[:], in0=rows["steep"][:], scalar=-1.0, in1=rows["share"][:], op0=ALU.mult, op1=ALU.mult
         )
 
-        gather_words(2)
-        round_w1(2, 0, 48)
-        quantise_w1(2, 0)
-        first_product([2], 0)
 
-        load_w1(2, 1)
-        load_vector("lean", lean)
+        round_w1(1, 0, P)
+        quantise_w1(1, 0)
+        w4_sc = kept([P, R_GROUPS * N], U8, "w4_sc")
+        nc.vector.tensor_copy(
+            out=w4_sc[:].rearrange("p (c t q) -> p c t q", t=PACK, q=P),
+            in_=w4_sc_raw[:].rearrange("p b (g q t) -> p (b g) t q", t=PACK, q=P),
+        )
+        gather_words(1, S)
+        first_product([1], 0)
+        round_w1(2, 0, P)
+        round_w1(0, 1, 0)
+        quantise_w1(2, 0)
+        quantise_w1(0, 1)
+        w4_w = kept([P, R_GROUPS * 2 * N], U8, "w4_w")
+        nc.scalar.copy(
+            out=w4_w[:].bitcast(U16).rearrange("p (c t q i) -> p c q t i", t=PACK, q=16, i=8),
+            in_=w4_raw[:].bitcast(U16).rearrange("p b (g q i t) -> p (b g) q t i", t=PACK, q=16, i=8),
+        )
         mix_sb = [load_rows(mix, b, "mix_sb") for b in range(R_GROUPS)]
         reach_sb = [load_rows(reach, g, "reach_sb") for g in range(N_GROUPS)]
+        gather_words(2, BANK)
+        first_product([2], 0)
+        round_w1(1, 1, P)
 
         factor = {ACT.Exp: neg_temp, ACT.Sigmoid: neg_gate}
-        round_w1(0, 1, P)
         leave_psum(0, ACT.Exp, pair_order[:4])
-        quantise_w1(0, 1)
-        leave_psum(0, ACT.Exp, pair_order[4:7])
-        round_w1(1, 1, 0)
-        leave_psum(0, ACT.Exp, pair_order[7:])
-        look(ACT.Exp, 0, M)
         first_product([0], 1)
         quantise_w1(1, 1)
+        leave_psum(0, ACT.Exp, pair_order[4:])
+        look(ACT.Exp, 0, M)
         first_product([1], 1)
         round_w1(2, 1, 0)
         vector_bias(0, ACT.Sigmoid, 0, PACK)
         quantise_w1(2, 1)
         first_product([2], 1)
         look(ACT.Sigmoid, 0, M)
-        leave_psum(1, ACT.Sigmoid, pair_order[:5])
-        vector_bias(1, ACT.Sigmoid, 0, 2)
-        leave_psum(1, ACT.Sigmoid, pair_order[5:])
-        vector_bias(1, ACT.Sigmoid, 2, PACK)
+        leave_psum(1, ACT.Sigmoid, pair_order)
+        vector_bias(1, ACT.Sigmoid, 0, PACK)
         vector_bias(1, ACT.Exp, 0, PACK)
         look(ACT.Sigmoid, 1, M)
         order_looks(0, slice(0, M))
@@ -379,7 +379,7 @@ def tile_list_order_book_looks_kernel(
         finish(1, 0, nc.scalar.copy)
         finish(1, 1, nc.vector.tensor_copy)
         for q in range(QUADS):
-            nc.sync.dma_start(
+            (nc.sync, nc.scalar)[q % 2].dma_start(
                 out=out_2[:, 4 * q : 4 * q + 4, :].rearrange("g r m -> r g m").bitcast(I32),
                 in_=y_s[32 * q : 32 * q + 4, :, :].bitcast(I32),
             )

@@ -111,12 +111,13 @@ def tile_list_order_book_looks_kernel(
 
         def round_w1(a, b, scalar_cols):
             grouped = w1_grouped[a, b] = work.tile([P, PASS * PACK], BF16, name="w1_grouped", align_bytes=64)
-            dst = grouped[:].rearrange("p (t m j) -> p m t j", t=PACK, j=PACK)
-            src = w1_raw[a, b][:].rearrange("p j (m t) -> p m t j", t=PACK)
+            dst = grouped[:].rearrange("p (u i m j) -> p u m j i", u=2, i=2, j=PACK)
+            src = w1_raw[a, b][:].rearrange("p j (m u i) -> p u m j i", u=2, i=2)
             if scalar_cols > 0:
-                nc.scalar.activation(out=dst[:, :scalar_cols], in_=src[:, :scalar_cols], func=ACT.Copy)
+                for u in (0, 1):
+                    nc.scalar.activation(out=dst[:, u, :scalar_cols], in_=src[:, u, :scalar_cols], func=ACT.Copy)
             if scalar_cols < P:
-                nc.vector.tensor_copy(out=dst[:, scalar_cols:], in_=src[:, scalar_cols:])
+                nc.vector.tensor_copy(out=dst[:, :, scalar_cols:], in_=src[:, :, scalar_cols:])
 
         def quantise_w1(a, b):
             w1_q[a, b] = kept([P, PASS], U32, "w1_q%d%d" % (a, b))
@@ -190,7 +191,6 @@ def tile_list_order_book_looks_kernel(
                         scale=scale[:, b * PACK + t : b * PACK + t + 1],
                     )
 
-        d_rows = {}
         halves = (slice(0, HALF), slice(HALF, M))
 
         low = {}
@@ -199,7 +199,6 @@ def tile_list_order_book_looks_kernel(
         def order_looks(b, cols):
             if cols.start == 0:
                 low[b] = tenant("low", [P, PACK, M], "low")
-                d_rows[b] = kept([P, PACK, M], BF16, "d_rows%d" % b)
             early, late = looked[ACT.Exp, b], looked[ACT.Sigmoid, b]
             for ts in pairs:
                 nc.vector.tensor_tensor(out=low[b][:, ts, cols], in0=early[:, ts, cols], in1=late[:, ts, cols], op=ALU.min)
@@ -213,7 +212,7 @@ def tile_list_order_book_looks_kernel(
                 )
             for t in range(PACK):
                 nc.vector.scalar_tensor_tensor(
-                    out=d_rows[b][:, t, cols],
+                    out=looked[ACT.Exp, b][:, t, cols],
                     in0=looked[ACT.Exp, b][:, t, cols],
                     scalar=rows["lean"][:, b * PACK + t : b * PACK + t + 1],
                     in1=low[b][:, t, cols],
@@ -224,8 +223,8 @@ def tile_list_order_book_looks_kernel(
         def interleave(src, copy):
             grouped = work.tile([P, HALF * PACK], BF16, name="grouped", bufs=3, align_bytes=64)
             copy(
-                out=grouped[:].rearrange("p (c i t) -> p c t i", i=4, t=PACK),
-                in_=src.rearrange("p t (c i) -> p c t i", i=4),
+                out=grouped[:].rearrange("p (c i t) -> p c t i", i=2, t=PACK),
+                in_=src.rearrange("p t (c i) -> p c t i", i=2),
             )
             return grouped
 
@@ -233,8 +232,8 @@ def tile_list_order_book_looks_kernel(
 
         d_q, d_s = {}, {}
 
-        def quantise_d(b, half):
-            grouped = interleave(d_rows[b][:, :, halves[half]], nc.scalar.copy)
+        def quantise_d(b, half, copy):
+            grouped = interleave(looked[ACT.Exp, b][:, :, halves[half]], copy)
             d_q[b, half] = kept([P, HALF], U32, "d_q%d%d" % (b, half))
             d_s[b, half] = kept([P, HALF], U8, "d_s%d%d" % (b, half))
             nc.vector.quantize_mx(out=d_q[b, half][:].bitcast(FP8X4), scales=d_s[b, half][:], in_=grouped[:])
@@ -261,7 +260,7 @@ def tile_list_order_book_looks_kernel(
         def finish(half, g, copy):
             cols = slice(half * HALF, (half + 1) * HALF)
             if g == 0:
-                y_half[half] = tenant("look%s0" % (half == 0), [P, N_GROUPS, PACK, HALF], "y")
+                y_half[half] = tenant("lookFalse%d" % half, [P, N_GROUPS, PACK, HALF], "y")
             y = y_half[half][:, g, :, :]
             for tp in (0, 1):
                 nc.vector.tensor_tensor(
@@ -291,30 +290,20 @@ def tile_list_order_book_looks_kernel(
         load_w1(1, 0)
         for q in range(QUADS):
             load_w4_scales(q)
-        load_tab(1)
-        load_w1(2, 0)
-        load_w1(0, 1)
         w4_raw = keep.tile([P, R_GROUPS, 2 * N], U8, name="w4_raw", tag="lookTrue0", align_bytes=64)
         nc.sync.dma_start(out=w4_raw[:].bitcast(I32), in_=w4_words.rearrange("b p n -> p b n").bitcast(I32))
+        load_tab(1)
         load_tab(2)
+        load_w1(2, 0)
+        load_w1(0, 1)
         load_w1(1, 1)
 
         got_sc = kept([P, S], U8, "got_sc")
         round_w1(0, 0, P)
         quantise_w1(0, 0)
-        load_w1(2, 1)
-        load_vector("lean", lean)
         gather_words(0, S)
         nc.vector.tensor_copy(got_sc[:], tab_sc[:].indirect(offs_sb[:]))
         first_product([0], 0)
-        neg_temp = kept([P, R_GROUPS * PACK], F32, "neg_temp")
-        neg_gate = kept([P, R_GROUPS * PACK], F32, "neg_gate")
-        nc.vector.tensor_scalar(out=neg_temp[:], in0=rows["temp"][:], scalar1=-1.0, scalar2=None, op0=ALU.mult)
-        nc.vector.scalar_tensor_tensor(
-            out=neg_gate[:], in0=rows["steep"][:], scalar=-1.0, in1=rows["share"][:], op0=ALU.mult, op1=ALU.mult
-        )
-
-
         round_w1(1, 0, P)
         quantise_w1(1, 0)
         w4_sc = kept([P, R_GROUPS * N], U8, "w4_sc")
@@ -322,37 +311,51 @@ def tile_list_order_book_looks_kernel(
             out=w4_sc[:].rearrange("p (c t q) -> p c t q", t=PACK, q=P),
             in_=w4_sc_raw[:].rearrange("p b (g q t) -> p (b g) t q", t=PACK, q=P),
         )
-        gather_words(1, S)
-        first_product([1], 0)
-        round_w1(2, 0, P)
-        round_w1(0, 1, 0)
-        quantise_w1(2, 0)
-        quantise_w1(0, 1)
         w4_w = kept([P, R_GROUPS * 2 * N], U8, "w4_w")
         nc.scalar.copy(
             out=w4_w[:].bitcast(U16).rearrange("p (c t q i) -> p c q t i", t=PACK, q=16, i=8),
             in_=w4_raw[:].bitcast(U16).rearrange("p b (g q i t) -> p (b g) q t i", t=PACK, q=16, i=8),
         )
+        gather_words(1, S)
+        first_product([1], 0)
+
+        neg_temp = kept([P, R_GROUPS * PACK], F32, "neg_temp")
+        neg_gate = kept([P, R_GROUPS * PACK], F32, "neg_gate")
+        nc.vector.tensor_scalar(out=neg_temp[:], in0=rows["temp"][:], scalar1=-1.0, scalar2=None, op0=ALU.mult)
+        nc.vector.scalar_tensor_tensor(
+            out=neg_gate[:], in0=rows["steep"][:], scalar=-1.0, in1=rows["share"][:], op0=ALU.mult, op1=ALU.mult
+        )
+
+        gather_words(2, S)
+        round_w1(2, 0, 48)
+        quantise_w1(2, 0)
+        first_product([2], 0)
+
+        load_w1(2, 1)
+        load_vector("lean", lean)
         mix_sb = [load_rows(mix, b, "mix_sb") for b in range(R_GROUPS)]
         reach_sb = [load_rows(reach, g, "reach_sb") for g in range(N_GROUPS)]
-        gather_words(2, BANK)
-        first_product([2], 0)
-        round_w1(1, 1, P)
 
         factor = {ACT.Exp: neg_temp, ACT.Sigmoid: neg_gate}
+        round_w1(0, 1, P)
         leave_psum(0, ACT.Exp, pair_order[:4])
+        quantise_w1(0, 1)
+        leave_psum(0, ACT.Exp, pair_order[4:7])
+        round_w1(1, 1, 0)
+        leave_psum(0, ACT.Exp, pair_order[7:])
+        look(ACT.Exp, 0, M)
         first_product([0], 1)
         quantise_w1(1, 1)
-        leave_psum(0, ACT.Exp, pair_order[4:])
-        look(ACT.Exp, 0, M)
         first_product([1], 1)
         round_w1(2, 1, 0)
         vector_bias(0, ACT.Sigmoid, 0, PACK)
         quantise_w1(2, 1)
         first_product([2], 1)
         look(ACT.Sigmoid, 0, M)
-        leave_psum(1, ACT.Sigmoid, pair_order)
-        vector_bias(1, ACT.Sigmoid, 0, PACK)
+        leave_psum(1, ACT.Sigmoid, pair_order[:5])
+        vector_bias(1, ACT.Sigmoid, 0, 2)
+        leave_psum(1, ACT.Sigmoid, pair_order[5:])
+        vector_bias(1, ACT.Sigmoid, 2, PACK)
         vector_bias(1, ACT.Exp, 0, PACK)
         look(ACT.Sigmoid, 1, M)
         order_looks(0, slice(0, M))
@@ -362,17 +365,17 @@ def tile_list_order_book_looks_kernel(
         order_looks(1, halves[0])
         combine(1, halves[0])
         order_looks(1, halves[1])
-        quantise_d(0, 0)
-        quantise_d(1, 0)
+        quantise_d(0, 0, nc.scalar.copy)
+        quantise_d(1, 0, nc.scalar.copy)
         for g in range(N_GROUPS):
             for b in range(R_GROUPS):
                 second_product(b, 0, g)
         combine(1, halves[1])
-        quantise_d(0, 1)
+        quantise_d(0, 1, nc.scalar.copy)
         for g in range(N_GROUPS):
             second_product(0, 1, g)
         finish(0, 0, nc.scalar.copy)
-        quantise_d(1, 1)
+        quantise_d(1, 1, nc.scalar.copy)
         for g in range(N_GROUPS):
             second_product(1, 1, g)
         finish(0, 1, nc.scalar.copy)

@@ -22,9 +22,13 @@ PASS = P * PACK
 K_PASSES = K // PASS
 R_GROUPS = H // PASS
 N_GROUPS = N // PASS
+PAIR = 2 * P
 BANK = 512
 HALF = M // 2
 QUADS = 4
+BLOCK = 8
+STAGE_BUFS = 5
+SCALAR_SHARE = 96
 
 
 def tile_list_order_book_looks_kernel(
@@ -34,18 +38,21 @@ def tile_list_order_book_looks_kernel(
     nc = tc.nc
     with ExitStack() as ctx:
         keep = ctx.enter_context(tc.tile_pool(name="keep", bufs=1))
-        stage = ctx.enter_context(tc.tile_pool(name="stage", bufs=5))
+        stage = ctx.enter_context(tc.tile_pool(name="stage", bufs=STAGE_BUFS))
         work = ctx.enter_context(tc.tile_pool(name="work", bufs=2))
         psum = ctx.enter_context(tc.psum_pool(name="psum", bufs=1))
 
         def kept(shape, dtype, name):
             return keep.tile(shape, dtype, name=name, align_bytes=64)
 
-        def staged(name):
-            return stage.tile([P, PACK, PASS], F32, name=name, tag="staged", align_bytes=64)
+        def staged(shape, dtype, name):
+            return stage.tile(shape, dtype, name=name, tag="staged", align_bytes=64)
 
-        def tenant(tag, shape, name):
-            return keep.tile(shape, F32, name=name, tag=tag, align_bytes=64)
+        def tenant(tag, shape, dtype, name):
+            return keep.tile(shape, dtype, name=name, tag=tag, align_bytes=64)
+
+        def look_tag(func, b):
+            return "%s%d" % ("early" if func == ACT.Exp else "late", b)
 
         def bank(i, name):
             return psum.tile([P, BANK], F32, name=name, tag="bank%d" % i)
@@ -54,11 +61,11 @@ def tile_list_order_book_looks_kernel(
         pos1_sb = keep.tile([P, M // 16], U16, name="pos1_sb")
         pos2_sb = keep.tile([P, M // 16], U16, name="pos2_sb")
 
-        tab_sc = kept([P, T], U8, "tab_sc")
+        tab_sc = tenant("tab_sc", [P, T], U8, "tab_sc")
         w4_sc_raw = kept([P, R_GROUPS, N], U8, "w4_sc_raw")
         nc.gpsimd.memset(tab_sc[:].bitcast(I32), 0)
         nc.vector.memset(w4_sc_raw[:].bitcast(I32), 0)
-        rows = {}
+        per_row = {}
 
         def load_tab_scales(q):
             nc.gpsimd.dma_start(
@@ -66,12 +73,21 @@ def tile_list_order_book_looks_kernel(
                 in_=tab_scales[:, 4 * q : 4 * q + 4, :].bitcast(I32),
             )
 
-        def load_vector(name, vec):
-            rows[name] = kept([P, R_GROUPS * PACK], F32, name + "_sb")
-            nc.sync.dma_start(
-                out=rows[name][:].rearrange("p (b t) -> p b t", t=PACK),
-                in_=vec.rearrange("(b p t) -> p b t", p=P, t=PACK),
-            )
+        def load_vector(name, vec, b):
+            if b == 0:
+                per_row[name, b] = kept([P, 2, BLOCK], F32, name + "0")
+                nc.sync.dma_start(
+                    out=per_row[name, b][:, :, 0:2], in_=vec[0:PASS].rearrange("(u p i) -> p u i", p=P, i=2)
+                )
+            else:
+                per_row[name, b] = kept([P, 2, 2], F32, name + "1")
+                nc.sync.dma_start(
+                    out=per_row[name, b][:].rearrange("p u i -> p (u i)"),
+                    in_=vec[PASS : 2 * PASS].rearrange("(p t) -> p t", t=PACK),
+                )
+
+        def row_value(name, b, t):
+            return per_row[name, b][:, t // 2, t % 2 : t % 2 + 1]
 
         def load_w4_scales(q):
             nc.sync.dma_start(
@@ -81,11 +97,14 @@ def tile_list_order_book_looks_kernel(
 
         w1_raw, tab, got = {}, {}, {}
 
-        def load_w1(a, b):
-            w1_raw[a, b] = staged("w1_raw")
+        def load_w1(a, c0, width, tag=None):
+            if tag is None:
+                w1_raw[a, c0] = staged([P, PACK, width], F32, "w1_raw")
+            else:
+                w1_raw[a, c0] = tenant(tag, [P, PACK, width], F32, "w1_raw")
             nc.sync.dma_start(
-                out=w1_raw[a, b][:],
-                in_=w1[a * PASS : (a + 1) * PASS, b * PASS : (b + 1) * PASS].rearrange("(p j) c -> p j c", j=PACK),
+                out=w1_raw[a, c0][:],
+                in_=w1[a * PASS : (a + 1) * PASS, c0 : c0 + width].rearrange("(p j) c -> p j c", j=PACK),
             )
 
         def load_tab(a):
@@ -93,112 +112,156 @@ def tile_list_order_book_looks_kernel(
             nc.sync.dma_start(out=tab[a][:], in_=tab_words[a].rearrange("p t i -> p (t i)").bitcast(I32))
 
         def load_rows(src, b, name):
-            dst = staged(name)
+            dst = staged([P, PACK, M], F32, name)
             nc.sync.dma_start(out=dst[:], in_=src[b * PASS : (b + 1) * PASS, :].rearrange("(p t) m -> p t m", t=PACK))
             return dst
 
         def gather_words(a, width):
-            got[a] = kept([P, S], U32, "got%d" % a)
+            if a == K_PASSES - 1:
+                got[a] = tenant("tab_sc", [P, S], U32, "got%d" % a)
+            else:
+                got[a] = kept([P, S], U32, "got%d" % a)
             for s0 in range(0, S, width):
                 nc.vector.tensor_copy(
                     got[a][:, s0 : s0 + width],
                     tab[a][:].bitcast(U32).indirect(offs_sb[:, s0 // 16 : (s0 + width) // 16]),
                 )
 
-        w1_q, w1_s = {}, {}
+        w1_q, w1_s, w1_grouped = {}, {}, {}
 
-        w1_grouped = {}
+        def round_pair(a, u):
+            if (a, u) == (1, 0):
+                grouped = tenant("got_sc", [P, PAIR * PACK], BF16, "w1_grouped")
+            else:
+                grouped = work.tile([P, PAIR * PACK], BF16, name="w1_grouped", align_bytes=64)
+            w1_grouped[a, u * PAIR] = grouped
+            nc.scalar.activation(
+                out=grouped[:].rearrange("p (i m j) -> p m j i", i=2, j=PACK),
+                in_=w1_raw[a, u * PAIR][:].rearrange("p j (m i) -> p m j i", i=2),
+                func=ACT.Copy,
+            )
 
-        def round_w1(a, b, scalar_cols):
-            grouped = w1_grouped[a, b] = work.tile([P, PASS * PACK], BF16, name="w1_grouped", align_bytes=64)
+        def group_views(a):
+            if a == 0:
+                grouped = work.tile([P, PASS * PACK], BF16, name="w1_grouped", align_bytes=64)
+            else:
+                grouped = tenant("w1_last", [P, PASS * PACK], BF16, "w1_grouped")
+            w1_grouped[a, PASS] = grouped
             dst = grouped[:].rearrange("p (u i m j) -> p u m j i", u=2, i=2, j=PACK)
-            src = w1_raw[a, b][:].rearrange("p j (m u i) -> p u m j i", u=2, i=2)
-            if scalar_cols > 0:
-                for u in (0, 1):
-                    nc.scalar.activation(out=dst[:, u, :scalar_cols], in_=src[:, u, :scalar_cols], func=ACT.Copy)
-            if scalar_cols < P:
-                nc.vector.tensor_copy(out=dst[:, :, scalar_cols:], in_=src[:, :, scalar_cols:])
+            src = w1_raw[a, PASS][:].rearrange("p j (m u i) -> p u m j i", u=2, i=2)
+            return dst, src
 
-        def quantise_w1(a, b):
-            w1_q[a, b] = kept([P, PASS], U32, "w1_q%d%d" % (a, b))
-            w1_s[a, b] = kept([P, PASS], U8, "w1_s%d%d" % (a, b))
-            nc.vector.quantize_mx(out=w1_q[a, b][:].bitcast(FP8X4), scales=w1_s[a, b][:], in_=w1_grouped[a, b][:])
+        def quantise_w1(a, c0, start, stop):
+            if start == 0:
+                width = PAIR if c0 < PASS else PASS
+                w1_q[a, c0] = kept([P, width], U32, "w1_q%d_%d" % (a, c0))
+                w1_s[a, c0] = kept([P, width], U8, "w1_s%d_%d" % (a, c0))
+            nc.vector.quantize_mx(
+                out=w1_q[a, c0][:, start:stop].bitcast(FP8X4),
+                scales=w1_s[a, c0][:, start:stop],
+                in_=w1_grouped[a, c0][:, start * PACK : stop * PACK],
+            )
 
         acc1 = {}
-        pair_order = [(t0 + dt, half) for t0 in (0, 2) for half in (0, 1) for dt in (0, 1)]
+        pair_banks = [[(2 * u + i, side) for side in (0, 1) for i in (0, 1)] for u in (0, 1)]
+        all_banks = pair_banks[0] + pair_banks[1]
 
-        def first_product(passes, b):
-            for t, half, a in [(t, half, a) for t, half in pair_order for a in passes]:
+        def first_product(a, b, banks):
+            for t, side in banks:
                 if a == 0:
-                    acc1[b, t, half] = bank(2 * t + half, "acc1")
-                cols = slice(half * BANK, (half + 1) * BANK)
+                    acc1[b, t, side] = bank(2 * t + side, "acc1")
+                c0, place = (PAIR * (t // 2), P * (t % 2)) if b == 0 else (PASS, P * t)
+                cols = slice(side * BANK, (side + 1) * BANK)
                 nc.tensor.matmul_mx(
-                    out=acc1[b, t, half][:],
-                    lhsT=w1_q[a, b][:, t * P : (t + 1) * P].bitcast(FP8X4),
-                    lhsT_scale=w1_s[a, b][:, t * P : (t + 1) * P],
+                    out=acc1[b, t, side][:],
+                    lhsT=w1_q[a, c0][:, place : place + P].bitcast(FP8X4),
+                    lhsT_scale=w1_s[a, c0][:, place : place + P],
                     rhs=got[a][:, cols].bitcast(FP8X4),
                     rhs_scale=got_sc[4 * a : P, cols],
                     start=(a == 0),
                     stop=(a == K_PASSES - 1),
                 )
 
-        h = {}
+        h, bias, top_side, pair_bias, group_bias, factor = {}, {}, {}, {}, {}, {}
         top = kept([P, R_GROUPS * PACK], F32, "top")
 
-        bias, top_half = {}, {}
-
-        def leave_psum(b, first, banks):
-            second = ACT.Sigmoid if first == ACT.Exp else ACT.Exp
-            for t, half in banks:
-                if (t, half) == (0, 0):
-                    bias[first, b] = tenant("look%s%d" % (second == ACT.Exp, b), [P, PACK], "first_bias")
-                    top_half[b] = tenant("low", [P, PACK], "top_half")
-                col = slice(b * PACK + t, b * PACK + t + 1)
-                if half == 0:
-                    h[b, t] = keep.tile([P, S], F32, name="h", tag="h%d%d" % (b, t), align_bytes=64)
+        def negated(func, b):
+            factor[func, b] = kept([P, PACK], F32, "factor_" + look_tag(func, b))
+            dst = factor[func, b][:].rearrange("p (u i) -> p u i", i=2)
+            if func == ACT.Exp:
                 nc.vector.tensor_scalar(
-                    out=h[b, t][:, half * BANK : (half + 1) * BANK],
-                    in0=acc1[b, t, half][:],
+                    out=dst, in0=per_row["temp", b][:, :, 0:2], scalar1=-1.0, scalar2=None, op0=ALU.mult
+                )
+            else:
+                nc.vector.scalar_tensor_tensor(
+                    out=dst, in0=per_row["steep", b][:, :, 0:2], scalar=-1.0, in1=per_row["share", b][:, :, 0:2],
+                    op0=ALU.mult, op1=ALU.mult,
+                )
+
+        def leave_psum(b, banks):
+            for t, side in banks:
+                if (t, side) == (0, 0):
+                    top_side[b] = tenant("low", [P, PACK], F32, "top_side")
+                col = slice(b * PACK + t, b * PACK + t + 1)
+                if side == 0:
+                    h[b, t] = tenant("h%d%d" % (b, t), [P, S], F32, "h%d%d" % (b, t))
+                nc.vector.tensor_scalar(
+                    out=h[b, t][:, side * BANK : (side + 1) * BANK],
+                    in0=acc1[b, t, side][:],
                     scalar1=1.0,
-                    scalar2=top_half[b][:, t : t + 1] if half else None,
+                    scalar2=top_side[b][:, t : t + 1] if side else None,
                     op0=ALU.mult,
                     op1=ALU.max,
-                    accum_out=top[:, col] if half else top_half[b][:, t : t + 1],
+                    accum_out=top[:, col] if side else top_side[b][:, t : t + 1],
                 )
-                if half and b == 0:
-                    nc.scalar.activation(
-                        out=bias[first, b][:, t : t + 1], in_=factor[first][:, col], func=ACT.Copy, scale=top[:, col]
-                    )
+                if side and b == 0:
+                    scalar_bias(t)
+
+        def scalar_bias(t):
+            if t % 2 == 0:
+                pair_bias[t // 2] = tenant(look_tag(ACT.Sigmoid, 1 - t // 2), [P, 2], F32, "pair_bias")
+            bias[ACT.Exp, 0, t] = pair_bias[t // 2][:, t % 2 : t % 2 + 1]
+            nc.scalar.activation(
+                out=bias[ACT.Exp, 0, t], in_=factor[ACT.Exp, 0][:, t : t + 1], func=ACT.Copy, scale=top[:, t : t + 1]
+            )
 
         def vector_bias(b, func, t0, t1):
-            if (func, b) not in bias:
-                bias[func, b] = kept([P, PACK], F32, "second_bias%d" % b)
-            group = slice(b * PACK + t0, b * PACK + t1)
-            nc.vector.tensor_tensor(out=bias[func, b][:, t0:t1], in0=factor[func][:, group], in1=top[:, group], op=ALU.mult)
+            if t0 == 0 and (func, b) == (ACT.Sigmoid, 1):
+                group_bias[func, b] = tenant(look_tag(ACT.Exp, 1), [P, PACK], F32, "group_bias")
+            elif t0 == 0:
+                group_bias[func, b] = kept([P, PACK], F32, "bias_" + look_tag(func, b))
+            for t in range(t0, t1):
+                bias[func, b, t] = group_bias[func, b][:, t : t + 1]
+            nc.vector.tensor_tensor(
+                out=group_bias[func, b][:, t0:t1],
+                in0=factor[func, b][:, t0:t1],
+                in1=top[:, b * PACK + t0 : b * PACK + t1],
+                op=ALU.mult,
+            )
 
         looked = {}
 
-        def look(func, b, width):
-            scale, pos = (rows["temp"], pos1_sb) if func == ACT.Exp else (rows["steep"], pos2_sb)
-            looked[func, b] = tenant("look%s%d" % (func == ACT.Exp, b), [P, PACK, M], "looked")
+        def look(func, b, width, slices):
+            scale, pos = ("temp", pos1_sb) if func == ACT.Exp else ("steep", pos2_sb)
+            if slices[0] == 0:
+                looked[func, b] = tenant(look_tag(func, b), [P, PACK, M], F32, "looked")
             for m0 in range(0, M, width):
-                for t in range(PACK):
+                for t in slices:
                     nc.scalar.activation(
                         out=looked[func, b][:, t, m0 : m0 + width],
                         in_=h[b, t][:].indirect(pos[:, m0 // 16 : (m0 + width) // 16]),
                         func=func,
-                        bias=bias[func, b][:, t : t + 1],
-                        scale=scale[:, b * PACK + t : b * PACK + t + 1],
+                        bias=bias[func, b, t],
+                        scale=row_value(scale, b, t),
                     )
 
         halves = (slice(0, HALF), slice(HALF, M))
-
-        low = {}
         pairs = (slice(0, 2), slice(2, 4))
+        low, d_rows, d_dealt = {}, {}, {}
 
         def order_looks(b, cols):
             if cols.start == 0:
-                low[b] = tenant("low", [P, PACK, M], "low")
+                low[b] = tenant("low", [P, PACK, M], F32, "low")
             early, late = looked[ACT.Exp, b], looked[ACT.Sigmoid, b]
             for ts in pairs:
                 nc.vector.tensor_tensor(out=low[b][:, ts, cols], in0=early[:, ts, cols], in1=late[:, ts, cols], op=ALU.min)
@@ -212,28 +275,26 @@ def tile_list_order_book_looks_kernel(
                 )
             for t in range(PACK):
                 nc.vector.scalar_tensor_tensor(
-                    out=looked[ACT.Exp, b][:, t, cols],
+                    out=d_rows[b][:, t, cols],
                     in0=looked[ACT.Exp, b][:, t, cols],
-                    scalar=rows["lean"][:, b * PACK + t : b * PACK + t + 1],
+                    scalar=row_value("lean", b, t),
                     in1=low[b][:, t, cols],
                     op0=ALU.mult,
                     op1=ALU.subtract,
                 )
 
-        def interleave(src, copy):
-            grouped = work.tile([P, HALF * PACK], BF16, name="grouped", bufs=3, align_bytes=64)
+        def interleave(src, copy, name):
+            grouped = work.tile([P, HALF * PACK], BF16, name=name, align_bytes=64)
             copy(
                 out=grouped[:].rearrange("p (c i t) -> p c t i", i=2, t=PACK),
                 in_=src.rearrange("p t (c i) -> p c t i", i=2),
             )
             return grouped
 
-        acc2 = {}
+        acc2, d_q, d_s = {}, {}, {}
 
-        d_q, d_s = {}, {}
-
-        def quantise_d(b, half, copy):
-            grouped = interleave(looked[ACT.Exp, b][:, :, halves[half]], copy)
+        def quantise_d(b, half):
+            grouped = interleave(d_dealt[b][:, :, halves[half]], nc.scalar.copy, "grouped")
             d_q[b, half] = kept([P, HALF], U32, "d_q%d%d" % (b, half))
             d_s[b, half] = kept([P, HALF], U8, "d_s%d%d" % (b, half))
             nc.vector.quantize_mx(out=d_q[b, half][:].bitcast(FP8X4), scales=d_s[b, half][:], in_=grouped[:])
@@ -254,128 +315,164 @@ def tile_list_order_book_looks_kernel(
                 )
 
         y_s = kept([P, N_GROUPS, M], U8, "y_s")
-
         y_half = {}
 
         def finish(half, g, copy):
-            cols = slice(half * HALF, (half + 1) * HALF)
+            cols = halves[half]
             if g == 0:
-                y_half[half] = tenant("lookFalse%d" % half, [P, N_GROUPS, PACK, HALF], "y")
+                y_half[half] = tenant(look_tag(ACT.Sigmoid, half), [P, N_GROUPS, PACK, HALF], F32, "y")
             y = y_half[half][:, g, :, :]
-            for tp in (0, 1):
+            for u in (0, 1):
                 nc.vector.tensor_tensor(
-                    out=y[:, 2 * tp : 2 * tp + 2, :],
-                    in0=acc2[half, g, tp][:].rearrange("p (t m) -> p t m", t=2),
-                    in1=reach_sb[g][:, 2 * tp : 2 * tp + 2, cols],
+                    out=y[:, pairs[u], :],
+                    in0=acc2[half, g, u][:].rearrange("p (i m) -> p i m", i=2),
+                    in1=reach_sb[g][:, pairs[u], cols],
                     op=ALU.mult,
                 )
             nc.sync.dma_start(
                 out=out_0[g * PASS : (g + 1) * PASS, cols].rearrange("(p t) m -> p t m", t=PACK), in_=y
             )
-            grouped = interleave(y, copy)
+            grouped = interleave(y, copy, "y_grouped")
             y_q = kept([P, HALF], I32, "y_q%d%d" % (half, g))
             nc.vector.quantize_mx(out=y_q[:].bitcast(FP8X4), scales=y_s[:, g, cols], in_=grouped[:])
             nc.sync.dma_start(out=out_1[g, :, cols, :].rearrange("p m t -> p (m t)").bitcast(I32), in_=y_q[:])
 
         for q in range(QUADS):
             load_tab_scales(q)
-        load_w1(0, 0)
+        load_w1(0, 0, PAIR)
         nc.sync.dma_start(offs_sb[:], offs)
-        load_vector("temp", temp)
-        load_vector("steep", steep)
-        load_vector("share", share)
-        nc.sync.dma_start(pos1_sb[:], pos1)
-        nc.sync.dma_start(pos2_sb[:], pos2)
         load_tab(0)
-        load_w1(1, 0)
+        load_w1(1, 0, PAIR)
+        load_vector("temp", temp, 0)
+        nc.sync.dma_start(pos1_sb[:], pos1)
+        load_tab(1)
+        load_w1(2, 0, PAIR)
         for q in range(QUADS):
             load_w4_scales(q)
-        w4_raw = keep.tile([P, R_GROUPS, 2 * N], U8, name="w4_raw", tag="lookTrue0", align_bytes=64)
-        nc.sync.dma_start(out=w4_raw[:].bitcast(I32), in_=w4_words.rearrange("b p n -> p b n").bitcast(I32))
-        load_tab(1)
         load_tab(2)
-        load_w1(2, 0)
-        load_w1(0, 1)
-        load_w1(1, 1)
+        load_w1(0, PAIR, PAIR)
+        load_w1(1, PAIR, PAIR)
 
-        got_sc = kept([P, S], U8, "got_sc")
-        round_w1(0, 0, P)
-        quantise_w1(0, 0)
+        round_pair(0, 0)
+        quantise_w1(0, 0, 0, PAIR)
+        load_w1(2, PAIR, PAIR, look_tag(ACT.Sigmoid, 1))
         gather_words(0, S)
+        round_pair(1, 0)
+        quantise_w1(1, 0, 0, PAIR)
+        load_w1(0, PASS, PASS)
+        got_sc = tenant("got_sc", [P, S], U8, "got_sc")
         nc.vector.tensor_copy(got_sc[:], tab_sc[:].indirect(offs_sb[:]))
-        first_product([0], 0)
-        round_w1(1, 0, P)
-        quantise_w1(1, 0)
+        first_product(0, 0, pair_banks[0])
+        gather_words(1, S)
+        first_product(1, 0, pair_banks[0])
+        round_pair(2, 0)
+        quantise_w1(2, 0, 0, PAIR)
+        load_w1(1, PASS, PASS, look_tag(ACT.Sigmoid, 0))
         w4_sc = kept([P, R_GROUPS * N], U8, "w4_sc")
         nc.vector.tensor_copy(
             out=w4_sc[:].rearrange("p (c t q) -> p c t q", t=PACK, q=P),
             in_=w4_sc_raw[:].rearrange("p b (g q t) -> p (b g) t q", t=PACK, q=P),
         )
-        w4_w = kept([P, R_GROUPS * 2 * N], U8, "w4_w")
-        nc.scalar.copy(
-            out=w4_w[:].bitcast(U16).rearrange("p (c t q i) -> p c q t i", t=PACK, q=16, i=8),
-            in_=w4_raw[:].bitcast(U16).rearrange("p b (g q i t) -> p (b g) q t i", t=PACK, q=16, i=8),
+        negated(ACT.Exp, 0)
+        gather_words(2, BANK)
+        first_product(2, 0, pair_banks[0])
+
+        round_pair(0, 1)
+        load_w1(2, PASS, PASS)
+        load_vector("steep", steep, 0)
+        load_vector("share", share, 0)
+        nc.sync.dma_start(pos2_sb[:], pos2)
+        for name, vec in (("temp", temp), ("steep", steep), ("share", share), ("lean", lean)):
+            load_vector(name, vec, 1)
+        load_vector("lean", lean, 0)
+        round_pair(1, 1)
+        round_pair(2, 1)
+        leave_psum(0, pair_banks[0][:1])
+        quantise_w1(0, PAIR, 0, PAIR)
+        first_product(0, 0, pair_banks[1])
+        leave_psum(0, pair_banks[0][1:3])
+        quantise_w1(1, PAIR, 0, PAIR)
+        first_product(1, 0, pair_banks[1])
+        leave_psum(0, pair_banks[0][3:])
+        look(ACT.Exp, 0, M, (0, 1))
+        quantise_w1(2, PAIR, 0, PAIR)
+        first_product(2, 0, pair_banks[1])
+        mix_sb = [staged([P, PACK, M], F32, "mix_sb")]
+        nc.sync.dma_start(
+            out=mix_sb[0][:].rearrange("p (u i) m -> p u i m", i=2),
+            in_=mix[0:PASS, :].rearrange("(u p i) m -> p u i m", p=P, i=2),
         )
-        gather_words(1, S)
-        first_product([1], 0)
+        mix_sb.append(load_rows(mix, 1, "mix_sb"))
 
-        neg_temp = kept([P, R_GROUPS * PACK], F32, "neg_temp")
-        neg_gate = kept([P, R_GROUPS * PACK], F32, "neg_gate")
-        nc.vector.tensor_scalar(out=neg_temp[:], in0=rows["temp"][:], scalar1=-1.0, scalar2=None, op0=ALU.mult)
-        nc.vector.scalar_tensor_tensor(
-            out=neg_gate[:], in0=rows["steep"][:], scalar=-1.0, in1=rows["share"][:], op0=ALU.mult, op1=ALU.mult
-        )
-
-        gather_words(2, S)
-        round_w1(2, 0, 48)
-        quantise_w1(2, 0)
-        first_product([2], 0)
-
-        load_w1(2, 1)
-        load_vector("lean", lean)
-        mix_sb = [load_rows(mix, b, "mix_sb") for b in range(R_GROUPS)]
-        reach_sb = [load_rows(reach, g, "reach_sb") for g in range(N_GROUPS)]
-
-        factor = {ACT.Exp: neg_temp, ACT.Sigmoid: neg_gate}
-        round_w1(0, 1, P)
-        leave_psum(0, ACT.Exp, pair_order[:4])
-        quantise_w1(0, 1)
-        leave_psum(0, ACT.Exp, pair_order[4:7])
-        round_w1(1, 1, 0)
-        leave_psum(0, ACT.Exp, pair_order[7:])
-        look(ACT.Exp, 0, M)
-        first_product([0], 1)
-        quantise_w1(1, 1)
-        first_product([1], 1)
-        round_w1(2, 1, 0)
+        dst, src = group_views(0)
+        nc.vector.tensor_copy(out=dst, in_=src)
+        leave_psum(0, pair_banks[1][:1])
+        quantise_w1(0, PASS, 0, PASS)
+        dst, src = group_views(1)
+        for u in (0, 1):
+            nc.scalar.activation(out=dst[:, u, :SCALAR_SHARE], in_=src[:, u, :SCALAR_SHARE], func=ACT.Copy)
+        nc.vector.tensor_copy(out=dst[:, :, SCALAR_SHARE:], in_=src[:, :, SCALAR_SHARE:])
+        leave_psum(0, pair_banks[1][1:])
+        look(ACT.Exp, 0, M, (2, 3))
+        w4_raw = staged([P, R_GROUPS, 2 * N], U8, "w4_raw")
+        nc.sync.dma_start(out=w4_raw[:].bitcast(I32), in_=w4_words.rearrange("b p n -> p b n").bitcast(I32))
+        first_product(0, 1, all_banks)
+        negated(ACT.Sigmoid, 0)
+        quantise_w1(1, PASS, 0, PASS)
+        first_product(1, 1, pair_banks[0])
+        dst, src = group_views(2)
+        for u in (0, 1):
+            nc.vector.tensor_copy(out=dst[:, u], in_=src[:, u])
+        quantise_w1(2, PASS, 0, PAIR)
+        first_product(2, 1, pair_banks[0])
+        first_product(1, 1, pair_banks[1])
+        quantise_w1(2, PASS, PAIR, PASS)
+        first_product(2, 1, pair_banks[1])
         vector_bias(0, ACT.Sigmoid, 0, PACK)
-        quantise_w1(2, 1)
-        first_product([2], 1)
-        look(ACT.Sigmoid, 0, M)
-        leave_psum(1, ACT.Sigmoid, pair_order[:5])
+        reach_sb = [load_rows(reach, g, "reach_sb") for g in range(N_GROUPS)]
+        negated(ACT.Sigmoid, 1)
+        negated(ACT.Exp, 1)
+        look(ACT.Sigmoid, 0, M, range(PACK))
+
+        leave_psum(1, all_banks[:5])
         vector_bias(1, ACT.Sigmoid, 0, 2)
-        leave_psum(1, ACT.Sigmoid, pair_order[5:])
+        leave_psum(1, all_banks[5:])
         vector_bias(1, ACT.Sigmoid, 2, PACK)
         vector_bias(1, ACT.Exp, 0, PACK)
-        look(ACT.Sigmoid, 1, M)
+        look(ACT.Sigmoid, 1, M, range(PACK))
+
         order_looks(0, slice(0, M))
+        d_rows[0] = kept([P, PACK, M], BF16, "d_rows0")
         combine(0, slice(0, M))
-        look(ACT.Exp, 1, HALF)
+        d_dealt[0] = kept([P, PACK, M], BF16, "d_dealt0")
+        for u in (0, 1):
+            nc.sync.dma_start(
+                out=d_dealt[0][u * P // 2 : (u + 1) * P // 2, :, :].rearrange("p (e i) m -> p e (i m)", i=2),
+                in_=d_rows[0][:, pairs[u], :].rearrange("p i m -> p (i m)"),
+            )
+        look(ACT.Exp, 1, HALF, range(PACK))
+        d_rows[1] = d_dealt[1] = looked[ACT.Exp, 1]
+
+        w4_w = tenant("h%d%d" % (R_GROUPS - 1, PACK - 1), [P, R_GROUPS * 2 * N], U8, "w4_w")
+        nc.scalar.copy(
+            out=w4_w[:].bitcast(U16).rearrange("p (c t o i) -> p c o t i", t=PACK, o=P // 8, i=8),
+            in_=w4_raw[:].bitcast(U16).rearrange("p b (g o i t) -> p (b g) o t i", t=PACK, o=P // 8, i=8),
+        )
 
         order_looks(1, halves[0])
         combine(1, halves[0])
         order_looks(1, halves[1])
-        quantise_d(0, 0, nc.scalar.copy)
-        quantise_d(1, 0, nc.scalar.copy)
+        quantise_d(0, 0)
+        quantise_d(1, 0)
         for g in range(N_GROUPS):
             for b in range(R_GROUPS):
                 second_product(b, 0, g)
         combine(1, halves[1])
-        quantise_d(0, 1, nc.scalar.copy)
+        quantise_d(0, 1)
         for g in range(N_GROUPS):
             second_product(0, 1, g)
         finish(0, 0, nc.scalar.copy)
-        quantise_d(1, 1, nc.scalar.copy)
+        quantise_d(1, 1)
         for g in range(N_GROUPS):
             second_product(1, 1, g)
         finish(0, 1, nc.scalar.copy)

from contextlib import ExitStack

import concourse.mybir as mybir

K, T, S, H, M, N = 1536, 4096, 1024, 1024, 512, 1024
FLOPS = 2 * K * H * S + 2 * H * N * M

F32 = mybir.dt.float32
BF16 = mybir.dt.bfloat16
I32 = mybir.dt.int32
U32 = mybir.dt.uint32
U16 = mybir.dt.uint16
U8 = mybir.dt.uint8
FP8X4 = mybir.dt.float8_e4m3fn_x4
FP4X4 = mybir.dt.float4_e2m1fn_x4
ALU = mybir.AluOpType
ACT = mybir.ActivationFunctionType

P = 128
PACK = 4
PASS = P * PACK
K_PASSES = K // PASS
R_GROUPS = H // PASS
N_GROUPS = N // PASS
PAIR = 2 * P
BANK = 512
HALF = M // 2
QUADS = 4
BLOCK = 8
STAGE_BUFS = 5
SCALAR_SHARE = 96


def tile_list_order_book_looks_kernel(
    tc, tab_words, tab_scales, offs, pos1, pos2, w1, temp, steep, share, lean, mix,
    w4_words, w4_scales, reach, out_0, out_1, out_2,
):
    nc = tc.nc
    with ExitStack() as ctx:
        keep = ctx.enter_context(tc.tile_pool(name="keep", bufs=1))
        stage = ctx.enter_context(tc.tile_pool(name="stage", bufs=STAGE_BUFS))
        work = ctx.enter_context(tc.tile_pool(name="work", bufs=2))
        psum = ctx.enter_context(tc.psum_pool(name="psum", bufs=1))

        def kept(shape, dtype, name):
            return keep.tile(shape, dtype, name=name, align_bytes=64)

        def staged(shape, dtype, name):
            return stage.tile(shape, dtype, name=name, tag="staged", align_bytes=64)

        def tenant(tag, shape, dtype, name):
            return keep.tile(shape, dtype, name=name, tag=tag, align_bytes=64)

        def look_tag(func, b):
            return "%s%d" % ("early" if func == ACT.Exp else "late", b)

        def bank(i, name):
            return psum.tile([P, BANK], F32, name=name, tag="bank%d" % i)

        offs_sb = keep.tile([P, S // 16], U16, name="offs_sb")
        pos1_sb = keep.tile([P, M // 16], U16, name="pos1_sb")
        pos2_sb = keep.tile([P, M // 16], U16, name="pos2_sb")

        tab_sc = tenant("tab_sc", [P, T], U8, "tab_sc")
        w4_sc_raw = kept([P, R_GROUPS, N], U8, "w4_sc_raw")
        nc.gpsimd.memset(tab_sc[:].bitcast(I32), 0)
        nc.vector.memset(w4_sc_raw[:].bitcast(I32), 0)
        per_row = {}

        def load_tab_scales(q):
            nc.gpsimd.dma_start(
                out=tab_sc[32 * q : 32 * q + 4 * K_PASSES, :].bitcast(I32),
                in_=tab_scales[:, 4 * q : 4 * q + 4, :].bitcast(I32),
            )

        def load_vector(name, vec, b):
            if b == 0:
                per_row[name, b] = kept([P, 2, BLOCK], F32, name + "0")
                nc.sync.dma_start(
                    out=per_row[name, b][:, :, 0:2], in_=vec[0:PASS].rearrange("(u p i) -> p u i", p=P, i=2)
                )
            else:
                per_row[name, b] = kept([P, 2, 2], F32, name + "1")
                nc.sync.dma_start(
                    out=per_row[name, b][:].rearrange("p u i -> p (u i)"),
                    in_=vec[PASS : 2 * PASS].rearrange("(p t) -> p t", t=PACK),
                )

        def row_value(name, b, t):
            return per_row[name, b][:, t // 2, t % 2 : t % 2 + 1]

        def load_w4_scales(q):
            nc.sync.dma_start(
                out=w4_sc_raw[32 * q : 32 * q + 4, :, :].bitcast(I32),
                in_=w4_scales[:, 4 * q : 4 * q + 4, :].rearrange("b r n -> r b n").bitcast(I32),
            )

        w1_raw, tab, got = {}, {}, {}

        def load_w1(a, c0, width, tag=None):
            if tag is None:
                w1_raw[a, c0] = staged([P, PACK, width], F32, "w1_raw")
            else:
                w1_raw[a, c0] = tenant(tag, [P, PACK, width], F32, "w1_raw")
            nc.sync.dma_start(
                out=w1_raw[a, c0][:],
                in_=w1[a * PASS : (a + 1) * PASS, c0 : c0 + width].rearrange("(p j) c -> p j c", j=PACK),
            )

        def load_tab(a):
            tab[a] = kept([P, T], I32, "tab%d" % a)
            nc.sync.dma_start(out=tab[a][:], in_=tab_words[a].rearrange("p t i -> p (t i)").bitcast(I32))

        def load_rows(src, b, name):
            dst = staged([P, PACK, M], F32, name)
            nc.sync.dma_start(out=dst[:], in_=src[b * PASS : (b + 1) * PASS, :].rearrange("(p t) m -> p t m", t=PACK))
            return dst

        def gather_words(a, width):
            if a == K_PASSES - 1:
                got[a] = tenant("tab_sc", [P, S], U32, "got%d" % a)
            else:
                got[a] = kept([P, S], U32, "got%d" % a)
            for s0 in range(0, S, width):
                nc.vector.tensor_copy(
                    got[a][:, s0 : s0 + width],
                    tab[a][:].bitcast(U32).indirect(offs_sb[:, s0 // 16 : (s0 + width) // 16]),
                )

        w1_q, w1_s, w1_grouped = {}, {}, {}

        def round_pair(a, u):
            if (a, u) == (1, 0):
                grouped = tenant("got_sc", [P, PAIR * PACK], BF16, "w1_grouped")
            else:
                grouped = work.tile([P, PAIR * PACK], BF16, name="w1_grouped", align_bytes=64)
            w1_grouped[a, u * PAIR] = grouped
            nc.scalar.activation(
                out=grouped[:].rearrange("p (i m j) -> p m j i", i=2, j=PACK),
                in_=w1_raw[a, u * PAIR][:].rearrange("p j (m i) -> p m j i", i=2),
                func=ACT.Copy,
            )

        def group_views(a):
            if a == 0:
                grouped = work.tile([P, PASS * PACK], BF16, name="w1_grouped", align_bytes=64)
            else:
                grouped = tenant("w1_last", [P, PASS * PACK], BF16, "w1_grouped")
            w1_grouped[a, PASS] = grouped
            dst = grouped[:].rearrange("p (u i m j) -> p u m j i", u=2, i=2, j=PACK)
            src = w1_raw[a, PASS][:].rearrange("p j (m u i) -> p u m j i", u=2, i=2)
            return dst, src

        def quantise_w1(a, c0, start, stop):
            if start == 0:
                width = PAIR if c0 < PASS else PASS
                w1_q[a, c0] = kept([P, width], U32, "w1_q%d_%d" % (a, c0))
                w1_s[a, c0] = kept([P, width], U8, "w1_s%d_%d" % (a, c0))
            nc.vector.quantize_mx(
                out=w1_q[a, c0][:, start:stop].bitcast(FP8X4),
                scales=w1_s[a, c0][:, start:stop],
                in_=w1_grouped[a, c0][:, start * PACK : stop * PACK],
            )

        acc1 = {}
        pair_banks = [[(2 * u + i, side) for side in (0, 1) for i in (0, 1)] for u in (0, 1)]
        all_banks = pair_banks[0] + pair_banks[1]

        def first_product(a, b, banks):
            for t, side in banks:
                if a == 0:
                    acc1[b, t, side] = bank(2 * t + side, "acc1")
                c0, place = (PAIR * (t // 2), P * (t % 2)) if b == 0 else (PASS, P * t)
                cols = slice(side * BANK, (side + 1) * BANK)
                nc.tensor.matmul_mx(
                    out=acc1[b, t, side][:],
                    lhsT=w1_q[a, c0][:, place : place + P].bitcast(FP8X4),
                    lhsT_scale=w1_s[a, c0][:, place : place + P],
                    rhs=got[a][:, cols].bitcast(FP8X4),
                    rhs_scale=got_sc[4 * a : P, cols],
                    start=(a == 0),
                    stop=(a == K_PASSES - 1),
                )

        h, bias, top_side, pair_bias, group_bias, factor = {}, {}, {}, {}, {}, {}
        top = kept([P, R_GROUPS * PACK], F32, "top")

        def negated(func, b):
            factor[func, b] = kept([P, PACK], F32, "factor_" + look_tag(func, b))
            dst = factor[func, b][:].rearrange("p (u i) -> p u i", i=2)
            if func == ACT.Exp:
                nc.vector.tensor_scalar(
                    out=dst, in0=per_row["temp", b][:, :, 0:2], scalar1=-1.0, scalar2=None, op0=ALU.mult
                )
            else:
                nc.vector.scalar_tensor_tensor(
                    out=dst, in0=per_row["steep", b][:, :, 0:2], scalar=-1.0, in1=per_row["share", b][:, :, 0:2],
                    op0=ALU.mult, op1=ALU.mult,
                )

        def leave_psum(b, banks):
            for t, side in banks:
                if (t, side) == (0, 0):
                    top_side[b] = tenant("low", [P, PACK], F32, "top_side")
                col = slice(b * PACK + t, b * PACK + t + 1)
                if side == 0:
                    h[b, t] = tenant("h%d%d" % (b, t), [P, S], F32, "h%d%d" % (b, t))
                nc.vector.tensor_scalar(
                    out=h[b, t][:, side * BANK : (side + 1) * BANK],
                    in0=acc1[b, t, side][:],
                    scalar1=1.0,
                    scalar2=top_side[b][:, t : t + 1] if side else None,
                    op0=ALU.mult,
                    op1=ALU.max,
                    accum_out=top[:, col] if side else top_side[b][:, t : t + 1],
                )
                if side and b == 0:
                    scalar_bias(t)

        def scalar_bias(t):
            if t % 2 == 0:
                pair_bias[t // 2] = tenant(look_tag(ACT.Sigmoid, 1 - t // 2), [P, 2], F32, "pair_bias")
            bias[ACT.Exp, 0, t] = pair_bias[t // 2][:, t % 2 : t % 2 + 1]
            nc.scalar.activation(
                out=bias[ACT.Exp, 0, t], in_=factor[ACT.Exp, 0][:, t : t + 1], func=ACT.Copy, scale=top[:, t : t + 1]
            )

        def vector_bias(b, func, t0, t1):
            if t0 == 0 and (func, b) == (ACT.Sigmoid, 1):
                group_bias[func, b] = tenant(look_tag(ACT.Exp, 1), [P, PACK], F32, "group_bias")
            elif t0 == 0:
                group_bias[func, b] = kept([P, PACK], F32, "bias_" + look_tag(func, b))
            for t in range(t0, t1):
                bias[func, b, t] = group_bias[func, b][:, t : t + 1]
            nc.vector.tensor_tensor(
                out=group_bias[func, b][:, t0:t1],
                in0=factor[func, b][:, t0:t1],
                in1=top[:, b * PACK + t0 : b * PACK + t1],
                op=ALU.mult,
            )

        looked = {}

        def look(func, b, width, slices):
            scale, pos = ("temp", pos1_sb) if func == ACT.Exp else ("steep", pos2_sb)
            if slices[0] == 0:
                looked[func, b] = tenant(look_tag(func, b), [P, PACK, M], F32, "looked")
            for m0 in range(0, M, width):
                for t in slices:
                    nc.scalar.activation(
                        out=looked[func, b][:, t, m0 : m0 + width],
                        in_=h[b, t][:].indirect(pos[:, m0 // 16 : (m0 + width) // 16]),
                        func=func,
                        bias=bias[func, b, t],
                        scale=row_value(scale, b, t),
                    )

        halves = (slice(0, HALF), slice(HALF, M))
        pairs = (slice(0, 2), slice(2, 4))
        low, d_rows, d_dealt = {}, {}, {}

        def order_looks(b, cols):
            if cols.start == 0:
                low[b] = tenant("low", [P, PACK, M], F32, "low")
            early, late = looked[ACT.Exp, b], looked[ACT.Sigmoid, b]
            for ts in pairs:
                nc.vector.tensor_tensor(out=low[b][:, ts, cols], in0=early[:, ts, cols], in1=late[:, ts, cols], op=ALU.min)
            for ts in pairs:
                nc.vector.tensor_tensor(out=early[:, ts, cols], in0=early[:, ts, cols], in1=late[:, ts, cols], op=ALU.max)

        def combine(b, cols):
            for ts in pairs:
                nc.vector.tensor_tensor(
                    out=low[b][:, ts, cols], in0=low[b][:, ts, cols], in1=mix_sb[b][:, ts, cols], op=ALU.mult
                )
            for t in range(PACK):
                nc.vector.scalar_tensor_tensor(
                    out=d_rows[b][:, t, cols],
                    in0=looked[ACT.Exp, b][:, t, cols],
                    scalar=row_value("lean", b, t),
                    in1=low[b][:, t, cols],
                    op0=ALU.mult,
                    op1=ALU.subtract,
                )

        def interleave(src, copy, name):
            grouped = work.tile([P, HALF * PACK], BF16, name=name, align_bytes=64)
            copy(
                out=grouped[:].rearrange("p (c i t) -> p c t i", i=2, t=PACK),
                in_=src.rearrange("p t (c i) -> p c t i", i=2),
            )
            return grouped

        acc2, d_q, d_s = {}, {}, {}

        def quantise_d(b, half):
            grouped = interleave(d_dealt[b][:, :, halves[half]], nc.scalar.copy, "grouped")
            d_q[b, half] = kept([P, HALF], U32, "d_q%d%d" % (b, half))
            d_s[b, half] = kept([P, HALF], U8, "d_s%d%d" % (b, half))
            nc.vector.quantize_mx(out=d_q[b, half][:].bitcast(FP8X4), scales=d_s[b, half][:], in_=grouped[:])

        def second_product(b, half, g):
            for t in range(PACK):
                if b == 0 and t % 2 == 0:
                    acc2[half, g, t // 2] = bank(4 * half + 2 * g + t // 2, "acc2")
                c0 = ((b * N_GROUPS + g) * PACK + t) * P
                nc.tensor.matmul_mx(
                    out=acc2[half, g, t // 2][:, (t % 2) * HALF : (t % 2 + 1) * HALF],
                    lhsT=w4_w[:, 2 * c0 : 2 * (c0 + P)].bitcast(FP4X4),
                    lhsT_scale=w4_sc[:, c0 : c0 + P],
                    rhs=d_q[b, half][:].bitcast(FP8X4),
                    rhs_scale=d_s[b, half][:],
                    start=(b == 0 and t % 2 == 0),
                    stop=(b == R_GROUPS - 1 and t % 2 == 1),
                )

        y_s = kept([P, N_GROUPS, M], U8, "y_s")
        y_half = {}

        def finish(half, g, copy):
            cols = halves[half]
            if g == 0:
                y_half[half] = tenant(look_tag(ACT.Sigmoid, half), [P, N_GROUPS, PACK, HALF], F32, "y")
            y = y_half[half][:, g, :, :]
            for u in (0, 1):
                nc.vector.tensor_tensor(
                    out=y[:, pairs[u], :],
                    in0=acc2[half, g, u][:].rearrange("p (i m) -> p i m", i=2),
                    in1=reach_sb[g][:, pairs[u], cols],
                    op=ALU.mult,
                )
            nc.sync.dma_start(
                out=out_0[g * PASS : (g + 1) * PASS, cols].rearrange("(p t) m -> p t m", t=PACK), in_=y
            )
            grouped = interleave(y, copy, "y_grouped")
            y_q = kept([P, HALF], I32, "y_q%d%d" % (half, g))
            nc.vector.quantize_mx(out=y_q[:].bitcast(FP8X4), scales=y_s[:, g, cols], in_=grouped[:])
            nc.sync.dma_start(out=out_1[g, :, cols, :].rearrange("p m t -> p (m t)").bitcast(I32), in_=y_q[:])

        for q in range(QUADS):
            load_tab_scales(q)
        load_w1(0, 0, PAIR)
        nc.sync.dma_start(offs_sb[:], offs)
        load_tab(0)
        load_w1(1, 0, PAIR)
        load_vector("temp", temp, 0)
        nc.sync.dma_start(pos1_sb[:], pos1)
        load_tab(1)
        load_w1(2, 0, PAIR)
        for q in range(QUADS):
            load_w4_scales(q)
        load_tab(2)
        load_w1(0, PAIR, PAIR)
        load_w1(1, PAIR, PAIR)

        round_pair(0, 0)
        quantise_w1(0, 0, 0, PAIR)
        load_w1(2, PAIR, PAIR, look_tag(ACT.Sigmoid, 1))
        gather_words(0, S)
        round_pair(1, 0)
        quantise_w1(1, 0, 0, PAIR)
        load_w1(0, PASS, PASS)
        got_sc = tenant("got_sc", [P, S], U8, "got_sc")
        nc.vector.tensor_copy(got_sc[:], tab_sc[:].indirect(offs_sb[:]))
        first_product(0, 0, pair_banks[0])
        gather_words(1, S)
        first_product(1, 0, pair_banks[0])
        round_pair(2, 0)
        quantise_w1(2, 0, 0, PAIR)
        load_w1(1, PASS, PASS, look_tag(ACT.Sigmoid, 0))
        w4_sc = kept([P, R_GROUPS * N], U8, "w4_sc")
        nc.vector.tensor_copy(
            out=w4_sc[:].rearrange("p (c t q) -> p c t q", t=PACK, q=P),
            in_=w4_sc_raw[:].rearrange("p b (g q t) -> p (b g) t q", t=PACK, q=P),
        )
        negated(ACT.Exp, 0)
        gather_words(2, BANK)
        first_product(2, 0, pair_banks[0])

        round_pair(0, 1)
        load_w1(2, PASS, PASS)
        load_vector("steep", steep, 0)
        load_vector("share", share, 0)
        nc.sync.dma_start(pos2_sb[:], pos2)
        for name, vec in (("temp", temp), ("steep", steep), ("share", share), ("lean", lean)):
            load_vector(name, vec, 1)
        load_vector("lean", lean, 0)
        round_pair(1, 1)
        round_pair(2, 1)
        leave_psum(0, pair_banks[0][:1])
        quantise_w1(0, PAIR, 0, PAIR)
        first_product(0, 0, pair_banks[1])
        leave_psum(0, pair_banks[0][1:3])
        quantise_w1(1, PAIR, 0, PAIR)
        first_product(1, 0, pair_banks[1])
        leave_psum(0, pair_banks[0][3:])
        look(ACT.Exp, 0, M, (0, 1))
        quantise_w1(2, PAIR, 0, PAIR)
        first_product(2, 0, pair_banks[1])
        mix_sb = [staged([P, PACK, M], F32, "mix_sb")]
        nc.sync.dma_start(
            out=mix_sb[0][:].rearrange("p (u i) m -> p u i m", i=2),
            in_=mix[0:PASS, :].rearrange("(u p i) m -> p u i m", p=P, i=2),
        )
        mix_sb.append(load_rows(mix, 1, "mix_sb"))

        dst, src = group_views(0)
        nc.vector.tensor_copy(out=dst, in_=src)
        leave_psum(0, pair_banks[1][:1])
        quantise_w1(0, PASS, 0, PASS)
        dst, src = group_views(1)
        for u in (0, 1):
            nc.scalar.activation(out=dst[:, u, :SCALAR_SHARE], in_=src[:, u, :SCALAR_SHARE], func=ACT.Copy)
        nc.vector.tensor_copy(out=dst[:, :, SCALAR_SHARE:], in_=src[:, :, SCALAR_SHARE:])
        leave_psum(0, pair_banks[1][1:])
        look(ACT.Exp, 0, M, (2, 3))
        w4_raw = staged([P, R_GROUPS, 2 * N], U8, "w4_raw")
        nc.sync.dma_start(out=w4_raw[:].bitcast(I32), in_=w4_words.rearrange("b p n -> p b n").bitcast(I32))
        first_product(0, 1, all_banks)
        negated(ACT.Sigmoid, 0)
        quantise_w1(1, PASS, 0, PASS)
        first_product(1, 1, pair_banks[0])
        dst, src = group_views(2)
        for u in (0, 1):
            nc.vector.tensor_copy(out=dst[:, u], in_=src[:, u])
        quantise_w1(2, PASS, 0, PAIR)
        first_product(2, 1, pair_banks[0])
        first_product(1, 1, pair_banks[1])
        quantise_w1(2, PASS, PAIR, PASS)
        first_product(2, 1, pair_banks[1])
        vector_bias(0, ACT.Sigmoid, 0, PACK)
        reach_sb = [load_rows(reach, g, "reach_sb") for g in range(N_GROUPS)]
        negated(ACT.Sigmoid, 1)
        negated(ACT.Exp, 1)
        look(ACT.Sigmoid, 0, M, range(PACK))

        leave_psum(1, all_banks[:5])
        vector_bias(1, ACT.Sigmoid, 0, 2)
        leave_psum(1, all_banks[5:])
        vector_bias(1, ACT.Sigmoid, 2, PACK)
        vector_bias(1, ACT.Exp, 0, PACK)
        look(ACT.Sigmoid, 1, M, range(PACK))

        order_looks(0, slice(0, M))
        d_rows[0] = kept([P, PACK, M], BF16, "d_rows0")
        combine(0, slice(0, M))
        d_dealt[0] = kept([P, PACK, M], BF16, "d_dealt0")
        for u in (0, 1):
            nc.sync.dma_start(
                out=d_dealt[0][u * P // 2 : (u + 1) * P // 2, :, :].rearrange("p (e i) m -> p e (i m)", i=2),
                in_=d_rows[0][:, pairs[u], :].rearrange("p i m -> p (i m)"),
            )
        look(ACT.Exp, 1, HALF, range(PACK))
        d_rows[1] = d_dealt[1] = looked[ACT.Exp, 1]

        w4_w = tenant("h%d%d" % (R_GROUPS - 1, PACK - 1), [P, R_GROUPS * 2 * N], U8, "w4_w")
        nc.scalar.copy(
            out=w4_w[:].bitcast(U16).rearrange("p (c t o i) -> p c o t i", t=PACK, o=P // 8, i=8),
            in_=w4_raw[:].bitcast(U16).rearrange("p b (g o i t) -> p (b g) o t i", t=PACK, o=P // 8, i=8),
        )

        order_looks(1, halves[0])
        combine(1, halves[0])
        order_looks(1, halves[1])
        quantise_d(0, 0)
        quantise_d(1, 0)
        for g in range(N_GROUPS):
            for b in range(R_GROUPS):
                second_product(b, 0, g)
        combine(1, halves[1])
        quantise_d(0, 1)
        for g in range(N_GROUPS):
            second_product(0, 1, g)
        finish(0, 0, nc.scalar.copy)
        quantise_d(1, 1)
        for g in range(N_GROUPS):
            second_product(1, 1, g)
        finish(0, 1, nc.scalar.copy)
        finish(1, 0, nc.scalar.copy)
        finish(1, 1, nc.vector.tensor_copy)
        for q in range(QUADS):
            (nc.sync, nc.scalar)[q % 2].dma_start(
                out=out_2[:, 4 * q : 4 * q + 4, :].rearrange("g r m -> r g m").bitcast(I32),
                in_=y_s[32 * q : 32 * q + 4, :, :].bitcast(I32),
            )
